import numpy as np
import ml_dtypes


def mxq(x, axis, fmt="e4m3"):
    dtype, down = {"e4m3": (ml_dtypes.float8_e4m3fn, 7), "e5m2": (ml_dtypes.float8_e5m2, 14)}[fmt]
    v = np.moveaxis(np.asarray(x, np.float32).astype(ml_dtypes.bfloat16).astype(np.float64), axis, -1)
    blocks = v.reshape(v.shape[:-1] + (-1, 32))
    amax = np.abs(blocks).max(-1, keepdims=True)
    byte = np.maximum(np.where(amax > 0, np.frexp(amax)[1] - 1 + 127, 0) - down, 1)
    scale = np.exp2(byte - 127.0)
    codes = (blocks / scale).astype(np.float32).astype(dtype).astype(np.float64)
    return np.moveaxis((codes * scale).reshape(v.shape), -1, axis)


WIDE = False


def mx_kscale(k, group=512):
    if not WIDE:
        return np.ones(k)
    levels = np.array([10, -10, 5, -5, 0])
    if group != 512:
        return np.exp2(np.random.permutation(np.resize(levels, k // group))).repeat(group)
    if k % 512:
        return np.exp2(np.random.permutation(np.resize(levels, k // 32))).repeat(32)
    a = np.empty((k // 512, 16))
    for p in range(k // 512):
        a[p, :8] = np.random.permutation(np.resize(levels, 8))
        for g in range(8):
            far = levels[np.abs(levels - a[p, g]) >= 10]
            a[p, g + 8] = far[np.random.randint(len(far))]
    return np.exp2(a.ravel()).repeat(32)


def f64(x):
    return np.asarray(x).astype(np.float64)


def striped(idx):
    return np.tile(np.asarray(idx).reshape(-1, 16).T, (8, 1)).astype(np.uint16)


def unstriped(offs):
    return offs[:16].T.reshape(-1).astype(np.int64)


H, KV, D, NQ, N = 4, 2, 256, 512, 512
CAP = 2.0


def setup_inputs():
    n = np.random.standard_normal
    s = mx_kscale(D, 0)[:, None]
    u = mx_kscale(N)
    t = np.random.uniform(0.5, 2.0, N) * u
    v = n((KV, N, 128))
    v[:, :, 127] = 1.0
    return {
        "qT": (n((H, D, NQ)) * s * (0.70 / np.sqrt(D))).astype(np.float32),
        "kT": (n((KV, D, N)) / s).astype(np.float32),
        "t": t.reshape(N, 1).astype(np.float32),
        "v": (v / t[:, None]).astype(np.float32),
        "mask": (np.arange(N)[:, None] <= np.sort(np.random.randint(N // 4, N, NQ))[None, :]).astype(np.float32),
    }


def reference(qT, kT, t, v, mask):
    a = np.repeat(mxq(f64(kT), 1, "e4m3"), H // KV, 0).transpose(0, 2, 1) @ mxq(f64(qT), 1, "e4m3")
    a = CAP * np.tanh(a / CAP)
    p = np.exp(a)
    p = p * f64(mask)
    w = p * f64(t)
    y = mxq(w, 1, "e4m3").transpose(0, 2, 1) @ np.repeat(mxq(f64(v), 1, "e4m3"), H // KV, 0)
    y = y / (y[:, :, 127:128])
    return y

@@ -1,0 +1,378 @@
+from contextlib import ExitStack
+
+import concourse.mybir as mybir
+
+F32 = mybir.dt.float32
+BF16 = mybir.dt.bfloat16
+U32 = mybir.dt.uint32
+U8 = mybir.dt.uint8
+FP8X4 = mybir.dt.float8_e4m3fn_x4
+ACT = mybir.ActivationFunctionType
+ALU = mybir.AluOpType
+
+H, KV, D, NQ, N, E = 4, 2, 256, 512, 512, 128
+CAP = 2.0
+P = 128
+PACK = 4
+ROWS = D // PACK
+QT = 128
+FLOPS = 2 * H * N * NQ * D + 2 * H * NQ * N * E
+PAIRS = ((1, 2), (0, 3))
+K_SPLIT = 44
+GROUPS = (
+    ((0, 0), (0, 1), (1, 0), (1, 1)),
+    ((2, 0), (2, 1), (3, 0), (3, 1)),
+    ((4, 0), (4, 1), (5, 0), (5, 1)),
+    ((6, 0), (6, 1)),
+    ((7, 0),),
+    ((7, 1),),
+)
+
+
+def tile_rows_a_exp_mask_cap_kernel(tc, qT, kT, t, v, mask, out):
+    nc = tc.nc
+    with ExitStack() as ctx:
+        sb = ctx.enter_context(tc.tile_pool(name="sb", bufs=1))
+        ps = ctx.enter_context(tc.psum_pool(name="ps", bufs=1))
+        ctx.enter_context(tc.manual_schedule())
+
+        def sbuf(name, shape, dtype):
+            return sb.tile(shape, dtype, name=name, align_bytes=64)
+
+        chunks = ((0, 0, 1), (0, 1, 1), (0, 2, 2), (1, 0, 2), (1, 2, 2))
+        q_raw = [sbuf("q_raw%d" % c, [P, PACK, n * QT], F32) for c, (a, j, n) in enumerate(chunks)]
+        q_bf = [sbuf("q_bf%d" % c, [P, n * QT, PACK], BF16) for c, (a, j, n) in enumerate(chunks)]
+        q_codes = [sbuf("q_codes%d" % c, [P, n * QT], U32) for c, (a, j, n) in enumerate(chunks)]
+        q_scales = [sbuf("q_scales%d" % c, [P, n * QT], U8) for c, (a, j, n) in enumerate(chunks)]
+        unit_chunk = {}
+        for c, (a, j, n) in enumerate(chunks):
+            for i in range(n):
+                unit_chunk[4 * a + j + i] = (c, i)
+
+        k_raw = [sbuf("k_raw%d" % hf, [P, PACK, N // 2], F32) for hf in range(2)]
+        k_bf = sbuf("k_bf", [P, PACK, P, PACK], BF16)
+        k_codes = sbuf("k_codes", [P, PACK, P], U32)
+        k_scales = sbuf("k_scales", [P, PACK, P], U8)
+        t_sb = sbuf("t_sb", [P, PACK], F32)
+        m_raw = [sbuf("m_raw%d" % hf, [P, PACK, NQ // 2], F32) for hf in range(2)]
+        mt = [sbuf("mt%d" % hf, [P, PACK, NQ // 2], F32) for hf in range(2)]
+        v_raw = sbuf("v_raw", [P, KV, PACK, E], F32)
+        v_bf = sbuf("v_bf", [P, KV, E, PACK], BF16)
+        v_codes = sbuf("v_codes", [P, KV * E], U32)
+        v_scales = sbuf("v_scales", [P, KV * E], U8)
+        th = [sbuf("th%d" % u, [P, KV, QT * PACK], F32) for u in range(8)]
+        pr = [sbuf("pr%d" % u, [P, KV, QT * PACK], F32) for u in range(8)]
+        w_bf = [sbuf("w_bf%d" % u, [P, KV, QT * PACK], BF16) for u in range(8)]
+        w_codes = [sbuf("w_codes%d" % u, [P, KV, QT], U32) for u in range(8)]
+        w_scales = [sbuf("w_scales%d" % u, [P, KV, QT], U8) for u in range(8)]
+        warm = sbuf("warm", [P, 2], F32)
+
+        place = {ug: (gi, i) for gi, members in enumerate(GROUPS) for i, ug in enumerate(members)}
+        recip = [sbuf("recip%d" % gi, [P, len(members)], F32) for gi, members in enumerate(GROUPS)]
+        res = [sbuf("res%d" % gi, [P, len(members), E], F32) for gi, members in enumerate(GROUPS)]
+        s_bank = {}
+        y_bank = {}
+
+        q_flat = qT.rearrange("h d q -> (h d) q")
+        k_view = kT.rearrange("g (p j) n -> (g p) j n", j=PACK)
+        m_view = mask.rearrange("(p r) q -> p r q", r=PACK)
+
+        def load_q(c):
+            a, j, n = chunks[c]
+            cols = slice(j * QT, (j + n) * QT)
+            lo, hi = PAIRS[a]
+            if hi == lo + 1:
+                rows = q_flat[lo * D : (hi + 1) * D, cols].rearrange("(p j) q -> p j q", j=PACK)
+                nc.sync.dma_start(out=q_raw[c][:], in_=rows)
+            else:
+                for g, h in enumerate(PAIRS[a]):
+                    rows = qT[h, :, cols].rearrange("(p j) q -> p j q", j=PACK)
+                    nc.sync.dma_start(out=q_raw[c][g * ROWS : (g + 1) * ROWS], in_=rows)
+
+        def load_k(hf):
+            nc.sync.dma_start(out=k_raw[hf][:], in_=k_view[:, :, hf * 256 : (hf + 1) * 256])
+
+        def load_m(hf):
+            nc.sync.dma_start(out=m_raw[hf][:], in_=m_view[:, :, hf * 256 : (hf + 1) * 256])
+
+        def load_v():
+            nc.sync.dma_start(
+                out=v_raw[:].rearrange("p g r e -> p g (r e)"),
+                in_=v.rearrange("g (p r) e -> p g (r e)", r=PACK),
+            )
+
+        def copy_q(c, on_scalar=False):
+            dst = q_bf[c][:].rearrange("p (c i) j -> p c j i", i=4)
+            src = q_raw[c][:].rearrange("p j (c i) -> p c j i", i=4)
+            if on_scalar:
+                nc.scalar.copy(out=dst, in_=src)
+            else:
+                nc.vector.tensor_copy(out=dst, in_=src)
+
+        def quant_q(c):
+            nc.vector.quantize_mx(
+                out=q_codes[c][:].bitcast(FP8X4),
+                scales=q_scales[c][:],
+                in_=q_bf[c][:].rearrange("p q j -> p (q j)"),
+            )
+
+        def copy_k(hf, s0, s1, on_scalar=False):
+            dst = k_bf[:, :, 64 * hf + s0 : 64 * hf + s1, :].rearrange("p r s j -> p s r j")
+            src = k_raw[hf][:, :, PACK * s0 : PACK * s1].rearrange("p j (s r) -> p s r j", r=PACK)
+            if on_scalar:
+                nc.scalar.copy(out=dst, in_=src)
+            else:
+                nc.vector.tensor_copy(out=dst, in_=src)
+
+        def quant_k(hf):
+            cols = slice(64 * hf, 64 * hf + 64)
+            for r in range(PACK):
+                nc.vector.quantize_mx(
+                    out=k_codes[:, r, cols].bitcast(FP8X4),
+                    scales=k_scales[:, r, cols],
+                    in_=k_bf[:, r, cols, :].rearrange("p s j -> p (s j)"),
+                )
+
+        def make_mt(hf):
+            for r in range(PACK):
+                nc.vector.tensor_scalar(
+                    out=mt[hf][:, r, :],
+                    in0=m_raw[hf][:, r, :],
+                    scalar1=t_sb[:, r : r + 1],
+                    scalar2=None,
+                    op0=ALU.mult,
+                )
+
+        def copy_v():
+            for g in range(KV):
+                nc.vector.tensor_copy(
+                    out=v_bf[:, g].rearrange("p (c i) r -> p c r i", i=4),
+                    in_=v_raw[:, g].rearrange("p r (c i) -> p c r i", i=4),
+                )
+
+        def quant_v():
+            nc.vector.quantize_mx(
+                out=v_codes[:].bitcast(FP8X4),
+                scales=v_scales[:],
+                in_=v_bf[:].rearrange("p g e r -> p (g e r)"),
+            )
+
+        def scores(u):
+            c, i = unit_chunk[u]
+            cols = slice(i * QT, (i + 1) * QT)
+            for g in range(KV):
+                s_bank[u, g] = ps.tile([P, PACK, QT], F32, name="s%d_%d" % (u, g), tag="s%d_%d" % (g, u % 2))
+            for r in range(PACK):
+                for g in range(KV):
+                    rows = slice(g * ROWS, (g + 1) * ROWS)
+                    nc.tensor.matmul_mx(
+                        out=s_bank[u, g][:, r, :],
+                        lhsT=k_codes[rows, r, :].bitcast(FP8X4),
+                        lhsT_scale=k_scales[rows, r, :],
+                        rhs=q_codes[c][rows, cols].bitcast(FP8X4),
+                        rhs_scale=q_scales[c][rows, cols],
+                        start=True,
+                        stop=True,
+                    )
+
+        def cap(u, g):
+            nc.scalar.activation(
+                out=th[u][:, g, :],
+                in_=s_bank[u, g][:].rearrange("p r q -> p (r q)"),
+                func=ACT.Tanh,
+                scale=1.0 / CAP,
+            )
+
+        def heads(g):
+            return slice(0, KV) if g is None else slice(g, g + 1)
+
+        def expo(u, g=None):
+            gs = heads(g)
+            nc.scalar.activation(out=pr[u][:, gs, :], in_=th[u][:, gs, :], func=ACT.Exp, scale=CAP)
+
+        def weigh(u, g=None):
+            gs = heads(g)
+            j = u % 4
+            m = mt[j // 2][:, :, (j % 2) * QT : (j % 2 + 1) * QT].rearrange("p r (c i) -> p c r i", i=2)
+            for x in range(gs.start, gs.stop):
+                nc.vector.tensor_tensor(
+                    out=w_bf[u][:, x, :].rearrange("p (c i r) -> p c r i", i=2, r=PACK),
+                    in0=pr[u][:, x, :].rearrange("p (r c i) -> p c r i", i=2, r=PACK),
+                    in1=m,
+                    op=ALU.mult,
+                )
+
+        def quant_w(u, g=None):
+            gs = heads(g)
+            nc.vector.quantize_mx(
+                out=w_codes[u][:, gs, :].rearrange("p g q -> p (g q)").bitcast(FP8X4),
+                scales=w_scales[u][:, gs, :].rearrange("p g q -> p (g q)"),
+                in_=w_bf[u][:, gs, :].rearrange("p g x -> p (g x)"),
+            )
+
+        def second(u, g=None):
+            gs = heads(g)
+            for x in range(gs.start, gs.stop):
+                gi, i = place[u, x]
+                if gi not in y_bank:
+                    y_bank[gi] = ps.tile([P, 2 * KV, E], F32, name="y%d" % gi, tag="y%d" % (gi % 4))
+                cols = slice(x * E, (x + 1) * E)
+                nc.tensor.matmul_mx(
+                    out=y_bank[gi][:, i, :],
+                    lhsT=w_codes[u][:, x, :].bitcast(FP8X4),
+                    lhsT_scale=w_scales[u][:, x, :],
+                    rhs=v_codes[:, cols].bitcast(FP8X4),
+                    rhs_scale=v_scales[:, cols],
+                    start=True,
+                    stop=True,
+                )
+
+        def invert(gi):
+            n = len(GROUPS[gi])
+            nc.vector.reciprocal(out=recip[gi][:], in_=y_bank[gi][:, 0:n, E - 1])
+
+        def divide(gi, on_scalar=False):
+            n = len(GROUPS[gi])
+            if on_scalar:
+                for x in range(n):
+                    nc.scalar.activation(
+                        out=res[gi][:, x, :], in_=y_bank[gi][:, x, :], func=ACT.Copy, scale=recip[gi][:, x : x + 1]
+                    )
+            else:
+                nc.vector.tensor_tensor(
+                    out=res[gi][:],
+                    in0=y_bank[gi][:, 0:n, :],
+                    in1=recip[gi][:].unsqueeze(2).to_broadcast([P, n, E]),
+                    op=ALU.mult,
+                )
+
+        def store(gi):
+            members = GROUPS[gi]
+            for i in range(0, len(members), KV):
+                u, g = members[i]
+                rows = slice((u % 4) * QT, (u % 4 + 1) * QT)
+                lo, hi = PAIRS[u // 4]
+                if len(members) == 1:
+                    nc.sync.dma_start(out=out[PAIRS[u // 4][g], rows, :], in_=res[gi][:, 0, :])
+                else:
+                    nc.sync.dma_start(
+                        out=out[lo : hi + 1 : hi - lo, rows, :].rearrange("g q e -> q g e"),
+                        in_=res[gi][:, i : i + KV, :],
+                    )
+
+        def load_t():
+            nc.scalar.dma_start(out=t_sb[:], in_=t.rearrange("(p r) o -> p (r o)", r=PACK))
+
+        def warm_up():
+            nc.vector.memset(warm[:, 0:1], 0.0)
+            nc.scalar.activation(out=warm[:, 1:2], in_=warm[:, 0:1], func=ACT.Exp)
+
+        load_k(0)
+        load_k(1)
+        load_t()
+        load_q(0)
+        load_q(1)
+        load_q(2)
+        load_m(0)
+        warm_up()
+        copy_k(0, 0, 64)
+        quant_k(0)
+        copy_k(1, 0, K_SPLIT)
+        copy_k(1, K_SPLIT, 64, on_scalar=True)
+        copy_q(0)
+        quant_k(1)
+        quant_q(0)
+        copy_q(1, on_scalar=True)
+        quant_q(1)
+        scores(0)
+        copy_q(2)
+        cap(0, 0)
+        scores(1)
+        quant_q(2)
+        cap(0, 1)
+        cap(1, 0)
+        make_mt(0)
+        expo(0)
+        load_q(3)
+        load_q(4)
+        weigh(0)
+        copy_q(3)
+        quant_q(3)
+        cap(1, 1)
+        scores(2)
+        cap(2, 0)
+        expo(1)
+        cap(2, 1)
+        scores(3)
+        cap(3, 0)
+        scores(4)
+        quant_w(0)
+        expo(2)
+        cap(3, 1)
+        weigh(1)
+        copy_q(4)
+        cap(4, 0)
+        load_m(1)
+        expo(3)
+        make_mt(1)
+        quant_q(4)
+        cap(4, 1)
+        scores(5)
+        weigh(2)
+        load_v()
+        cap(5, 0)
+        copy_v()
+        scores(6)
+        weigh(3)
+        expo(4)
+        quant_w(1)
+        quant_w(2)
+        quant_v()
+        second(0)
+        second(1)
+        cap(5, 1)
+        second(2)
+        cap(6, 0)
+        scores(7)
+        expo(5)
+        weigh(4)
+        quant_w(3)
+        cap(6, 1)
+        invert(0)
+        quant_w(4)
+        divide(0)
+        weigh(5)
+        cap(7, 0)
+        second(3)
+        quant_w(5)
+        expo(6)
+        second(4)
+        invert(1)
+        second(5)
+        weigh(6)
+        cap(7, 1)
+        store(0)
+        expo(7, 0)
+        weigh(7, 0)
+        invert(2)
+        quant_w(6)
+        expo(7, 1)
+        divide(1, on_scalar=True)
+        divide(2, on_scalar=True)
+        quant_w(7, 0)
+        second(6)
+        second(7, 0)
+        store(1)
+        weigh(7, 1)
+        invert(3)
+        store(2)
+        quant_w(7, 1)
+        divide(3)
+        store(3)
+        second(7, 1)
+        invert(4)
+        invert(5)
+        divide(4)
+        divide(5)
+        store(4)
+        store(5)

@@ -18,7 +18,8 @@ ROWS = D // PACK
 QT = 128
 FLOPS = 2 * H * N * NQ * D + 2 * H * NQ * N * E
 PAIRS = ((1, 2), (0, 3))
-K_SPLIT = 44
+K_SPLIT = 118
+K_CHUNKS = ((0, 96), (96, 128))
 GROUPS = (
     ((0, 0), (0, 1), (1, 0), (1, 1)),
     ((2, 0), (2, 1), (3, 0), (3, 1)),
@@ -39,23 +40,18 @@ def tile_rows_a_exp_mask_cap_kernel(tc, qT, kT, t, v, mask, out):
         def sbuf(name, shape, dtype):
             return sb.tile(shape, dtype, name=name, align_bytes=64)
 
-        chunks = ((0, 0, 1), (0, 1, 1), (0, 2, 2), (1, 0, 2), (1, 2, 2))
-        q_raw = [sbuf("q_raw%d" % c, [P, PACK, n * QT], F32) for c, (a, j, n) in enumerate(chunks)]
-        q_bf = [sbuf("q_bf%d" % c, [P, n * QT, PACK], BF16) for c, (a, j, n) in enumerate(chunks)]
-        q_codes = [sbuf("q_codes%d" % c, [P, n * QT], U32) for c, (a, j, n) in enumerate(chunks)]
-        q_scales = [sbuf("q_scales%d" % c, [P, n * QT], U8) for c, (a, j, n) in enumerate(chunks)]
-        unit_chunk = {}
-        for c, (a, j, n) in enumerate(chunks):
-            for i in range(n):
-                unit_chunk[4 * a + j + i] = (c, i)
+        q_raw = [sbuf("q_raw%d" % a, [P, PACK, NQ], F32) for a in range(2)]
+        q_bf = sbuf("q_bf", [P, 2 * NQ, PACK], BF16)
+        q_codes = sbuf("q_codes", [P, 2 * NQ], U32)
+        q_scales = sbuf("q_scales", [P, 2 * NQ], U8)
 
-        k_raw = [sbuf("k_raw%d" % hf, [P, PACK, N // 2], F32) for hf in range(2)]
+        k_raw = sbuf("k_raw", [P, PACK, N], F32)
         k_bf = sbuf("k_bf", [P, PACK, P, PACK], BF16)
         k_codes = sbuf("k_codes", [P, PACK, P], U32)
         k_scales = sbuf("k_scales", [P, PACK, P], U8)
         t_sb = sbuf("t_sb", [P, PACK], F32)
-        m_raw = [sbuf("m_raw%d" % hf, [P, PACK, NQ // 2], F32) for hf in range(2)]
-        mt = [sbuf("mt%d" % hf, [P, PACK, NQ // 2], F32) for hf in range(2)]
+        m_raw = sbuf("m_raw", [P, PACK, NQ], F32)
+        mt = sbuf("mt", [P, PACK, NQ], F32)
         v_raw = sbuf("v_raw", [P, KV, PACK, E], F32)
         v_bf = sbuf("v_bf", [P, KV, E, PACK], BF16)
         v_codes = sbuf("v_codes", [P, KV * E], U32)
@@ -77,23 +73,24 @@ def tile_rows_a_exp_mask_cap_kernel(tc, qT, kT, t, v, mask, out):
         k_view = kT.rearrange("g (p j) n -> (g p) j n", j=PACK)
         m_view = mask.rearrange("(p r) q -> p r q", r=PACK)
 
-        def load_q(c):
-            a, j, n = chunks[c]
+        def load_q(a, j, n):
             cols = slice(j * QT, (j + n) * QT)
             lo, hi = PAIRS[a]
             if hi == lo + 1:
                 rows = q_flat[lo * D : (hi + 1) * D, cols].rearrange("(p j) q -> p j q", j=PACK)
-                nc.sync.dma_start(out=q_raw[c][:], in_=rows)
+                nc.sync.dma_start(out=q_raw[a][:, :, cols], in_=rows)
             else:
                 for g, h in enumerate(PAIRS[a]):
                     rows = qT[h, :, cols].rearrange("(p j) q -> p j q", j=PACK)
-                    nc.sync.dma_start(out=q_raw[c][g * ROWS : (g + 1) * ROWS], in_=rows)
+                    nc.sync.dma_start(out=q_raw[a][g * ROWS : (g + 1) * ROWS, :, cols], in_=rows)
 
-        def load_k(hf):
-            nc.sync.dma_start(out=k_raw[hf][:], in_=k_view[:, :, hf * 256 : (hf + 1) * 256])
+        def load_k(c):
+            cols = slice(PACK * K_CHUNKS[c][0], PACK * K_CHUNKS[c][1])
+            nc.sync.dma_start(out=k_raw[:, :, cols], in_=k_view[:, :, cols])
 
-        def load_m(hf):
-            nc.sync.dma_start(out=m_raw[hf][:], in_=m_view[:, :, hf * 256 : (hf + 1) * 256])
+        def load_m(j, n):
+            cols = slice(j * QT, (j + n) * QT)
+            nc.sync.dma_start(out=m_raw[:, :, cols], in_=m_view[:, :, cols])
 
         def load_v():
             nc.sync.dma_start(
@@ -101,24 +98,25 @@ def tile_rows_a_exp_mask_cap_kernel(tc, qT, kT, t, v, mask, out):
                 in_=v.rearrange("g (p r) e -> p g (r e)", r=PACK),
             )
 
-        def copy_q(c, on_scalar=False):
-            dst = q_bf[c][:].rearrange("p (c i) j -> p c j i", i=4)
-            src = q_raw[c][:].rearrange("p j (c i) -> p c j i", i=4)
+        def copy_q(u, n, on_scalar=False):
+            dst = q_bf[:, u * QT : (u + n) * QT, :].rearrange("p (c i) j -> p c j i", i=4)
+            src = q_raw[u // 4][:, :, (u % 4) * QT : (u % 4 + n) * QT].rearrange("p j (c i) -> p c j i", i=4)
             if on_scalar:
                 nc.scalar.copy(out=dst, in_=src)
             else:
                 nc.vector.tensor_copy(out=dst, in_=src)
 
-        def quant_q(c):
+        def quant_q(u, n):
+            cols = slice(u * QT, (u + n) * QT)
             nc.vector.quantize_mx(
-                out=q_codes[c][:].bitcast(FP8X4),
-                scales=q_scales[c][:],
-                in_=q_bf[c][:].rearrange("p q j -> p (q j)"),
+                out=q_codes[:, cols].bitcast(FP8X4),
+                scales=q_scales[:, cols],
+                in_=q_bf[:, cols, :].rearrange("p q j -> p (q j)"),
             )
 
-        def copy_k(hf, s0, s1, on_scalar=False):
-            dst = k_bf[:, :, 64 * hf + s0 : 64 * hf + s1, :].rearrange("p r s j -> p s r j")
-            src = k_raw[hf][:, :, PACK * s0 : PACK * s1].rearrange("p j (s r) -> p s r j", r=PACK)
+        def copy_k(c, s0, s1, on_scalar=False):
+            dst = k_bf[:, :, s0:s1, :].rearrange("p r s j -> p s r j")
+            src = k_raw[:, :, PACK * s0 : PACK * s1].rearrange("p j (s r) -> p s r j", r=PACK)
             if on_scalar:
                 nc.scalar.copy(out=dst, in_=src)
             else:
@@ -133,11 +131,12 @@ def tile_rows_a_exp_mask_cap_kernel(tc, qT, kT, t, v, mask, out):
                     in_=k_bf[:, r, cols, :].rearrange("p s j -> p (s j)"),
                 )
 
-        def make_mt(hf):
+        def make_mt(j, n):
+            cols = slice(j * QT, (j + n) * QT)
             for r in range(PACK):
                 nc.vector.tensor_scalar(
-                    out=mt[hf][:, r, :],
-                    in0=m_raw[hf][:, r, :],
+                    out=mt[:, r, cols],
+                    in0=m_raw[:, r, cols],
                     scalar1=t_sb[:, r : r + 1],
                     scalar2=None,
                     op0=ALU.mult,
@@ -158,8 +157,7 @@ def tile_rows_a_exp_mask_cap_kernel(tc, qT, kT, t, v, mask, out):
             )
 
         def scores(u):
-            c, i = unit_chunk[u]
-            cols = slice(i * QT, (i + 1) * QT)
+            cols = slice(u * QT, (u + 1) * QT)
             for g in range(KV):
                 s_bank[u, g] = ps.tile([P, PACK, QT], F32, name="s%d_%d" % (u, g), tag="s%d_%d" % (g, u % 2))
             for r in range(PACK):
@@ -169,8 +167,8 @@ def tile_rows_a_exp_mask_cap_kernel(tc, qT, kT, t, v, mask, out):
                         out=s_bank[u, g][:, r, :],
                         lhsT=k_codes[rows, r, :].bitcast(FP8X4),
                         lhsT_scale=k_scales[rows, r, :],
-                        rhs=q_codes[c][rows, cols].bitcast(FP8X4),
-                        rhs_scale=q_scales[c][rows, cols],
+                        rhs=q_codes[rows, cols].bitcast(FP8X4),
+                        rhs_scale=q_scales[rows, cols],
                         start=True,
                         stop=True,
                     )
@@ -193,7 +191,7 @@ def tile_rows_a_exp_mask_cap_kernel(tc, qT, kT, t, v, mask, out):
         def weigh(u, g=None):
             gs = heads(g)
             j = u % 4
-            m = mt[j // 2][:, :, (j % 2) * QT : (j % 2 + 1) * QT].rearrange("p r (c i) -> p c r i", i=2)
+            m = mt[:, :, j * QT : (j + 1) * QT].rearrange("p r (c i) -> p c r i", i=2)
             for x in range(gs.start, gs.stop):
                 nc.vector.tensor_tensor(
                     out=w_bf[u][:, x, :].rearrange("p (c i r) -> p c r i", i=2, r=PACK),
@@ -201,6 +199,26 @@ def tile_rows_a_exp_mask_cap_kernel(tc, qT, kT, t, v, mask, out):
                     in1=m,
                     op=ALU.mult,
                 )
+
+        def expo_half(u, g, hf):
+            cols = slice(hf * QT // 2, (hf + 1) * QT // 2)
+            nc.scalar.activation(
+                out=pr[u][:, g, :].rearrange("p (r q) -> p r q", r=PACK)[:, :, cols],
+                in_=th[u][:, g, :].rearrange("p (r q) -> p r q", r=PACK)[:, :, cols],
+                func=ACT.Exp,
+                scale=CAP,
+            )
+
+        def weigh_half(u, g, hf):
+            j = u % 4
+            pairs = slice(hf * QT // 4, (hf + 1) * QT // 4)
+            m = mt[:, :, j * QT : (j + 1) * QT].rearrange("p r (c i) -> p c r i", i=2)
+            nc.vector.tensor_tensor(
+                out=w_bf[u][:, g, :].rearrange("p (c i r) -> p c r i", i=2, r=PACK)[:, pairs],
+                in0=pr[u][:, g, :].rearrange("p (r c i) -> p c r i", i=2, r=PACK)[:, pairs],
+                in1=m[:, pairs],
+                op=ALU.mult,
+            )
 
         def quant_w(u, g=None):
             gs = heads(g)
@@ -268,111 +286,114 @@ def tile_rows_a_exp_mask_cap_kernel(tc, qT, kT, t, v, mask, out):
             nc.scalar.activation(out=warm[:, 1:2], in_=warm[:, 0:1], func=ACT.Exp)
 
         load_k(0)
+        load_q(0, 0, 1)
         load_k(1)
+        load_q(0, 1, 1)
+        load_q(0, 2, 2)
+        load_m(0, 2)
+        load_v()
+        load_q(1, 0, 2)
+        load_m(2, 2)
+        load_q(1, 2, 2)
         load_t()
-        load_q(0)
-        load_q(1)
-        load_q(2)
-        load_m(0)
         warm_up()
         copy_k(0, 0, 64)
+        copy_k(0, 64, 96, on_scalar=True)
+        copy_q(0, 1)
         quant_k(0)
-        copy_k(1, 0, K_SPLIT)
-        copy_k(1, K_SPLIT, 64, on_scalar=True)
-        copy_q(0)
+        quant_q(0, 1)
+        copy_k(1, 96, K_SPLIT)
+        copy_k(1, K_SPLIT, 128, on_scalar=True)
         quant_k(1)
-        quant_q(0)
-        copy_q(1, on_scalar=True)
-        quant_q(1)
         scores(0)
-        copy_q(2)
         cap(0, 0)
+        copy_q(1, 1)
+        quant_q(1, 1)
         scores(1)
-        quant_q(2)
+        copy_q(2, 2)
         cap(0, 1)
         cap(1, 0)
-        make_mt(0)
-        expo(0)
-        load_q(3)
-        load_q(4)
-        weigh(0)
-        copy_q(3)
-        quant_q(3)
-        cap(1, 1)
+        quant_q(2, 2)
         scores(2)
+        make_mt(0, 2)
+        expo(0)
+        cap(1, 1)
+        weigh(0)
+        copy_v()
         cap(2, 0)
         expo(1)
         cap(2, 1)
         scores(3)
-        cap(3, 0)
-        scores(4)
         quant_w(0)
-        expo(2)
-        cap(3, 1)
         weigh(1)
-        copy_q(4)
-        cap(4, 0)
-        load_m(1)
-        expo(3)
-        make_mt(1)
-        quant_q(4)
-        cap(4, 1)
-        scores(5)
-        weigh(2)
-        load_v()
-        cap(5, 0)
-        copy_v()
-        scores(6)
-        weigh(3)
-        expo(4)
+        cap(3, 0)
+        copy_q(4, 2)
+        cap(3, 1)
         quant_w(1)
-        quant_w(2)
+        quant_q(4, 2)
+        make_mt(2, 2)
+        expo(2)
         quant_v()
+        scores(4)
+        expo(3)
+        cap(4, 0)
+        cap(4, 1)
+        weigh(2)
+        weigh(3)
+        copy_q(6, 2)
+        quant_w(2)
+        scores(5)
         second(0)
-        second(1)
+        cap(5, 0)
         cap(5, 1)
-        second(2)
+        second(1)
+        quant_q(6, 2)
+        scores(6)
+        invert(0)
+        expo(4)
+        quant_w(3)
+        weigh(4)
+        expo(5)
         cap(6, 0)
         scores(7)
-        expo(5)
-        weigh(4)
-        quant_w(3)
-        cap(6, 1)
-        invert(0)
-        quant_w(4)
-        divide(0)
         weigh(5)
+        quant_w(4)
+        cap(6, 1)
+        quant_w(5)
+        second(2)
         cap(7, 0)
         second(3)
-        quant_w(5)
-        expo(6)
-        second(4)
         invert(1)
-        second(5)
-        weigh(6)
+        divide(0)
+        expo(6)
         cap(7, 1)
-        store(0)
+        second(4)
+        second(5)
         expo(7, 0)
-        weigh(7, 0)
-        invert(2)
-        quant_w(6)
-        expo(7, 1)
+        store(0)
+        expo_half(7, 1, 0)
+        weigh(6)
         divide(1, on_scalar=True)
-        divide(2, on_scalar=True)
-        quant_w(7, 0)
+        invert(2)
+        weigh(7, 0)
+        quant_w(6)
         second(6)
-        second(7, 0)
         store(1)
-        weigh(7, 1)
+        expo_half(7, 1, 1)
+        weigh_half(7, 1, 0)
+        weigh_half(7, 1, 1)
+        quant_w(7, 0)
         invert(3)
+        second(7, 0)
+        divide(2, on_scalar=True)
         store(2)
         quant_w(7, 1)
-        divide(3)
-        store(3)
         second(7, 1)
         invert(4)
+        divide(3, on_scalar=True)
         invert(5)
+        store(3)
         divide(4)
-        divide(5)
         store(4)
+        divide(5)
         store(5)

@@ -18,16 +18,10 @@ ROWS = D // PACK
 QT = 128
 FLOPS = 2 * H * N * NQ * D + 2 * H * NQ * N * E
 PAIRS = ((1, 2), (0, 3))
-K_SPLIT = 118
-K_CHUNKS = ((0, 96), (96, 128))
-GROUPS = (
-    ((0, 0), (0, 1), (1, 0), (1, 1)),
-    ((2, 0), (2, 1), (3, 0), (3, 1)),
-    ((4, 0), (4, 1), (5, 0), (5, 1)),
-    ((6, 0), (6, 1)),
-    ((7, 0),),
-    ((7, 1),),
-)
+UNITS = 8
+JOBS = 2 * UNITS
+K_SPLIT = 40
+GROUPS = ((0, 1, 2, 3), (4, 5, 6, 7), (8, 9, 10, 11), (12, 13), (14,), (15,))
 
 
 def tile_rows_a_exp_mask_cap_kernel(tc, qT, kT, t, v, mask, out):
@@ -40,30 +34,28 @@ def tile_rows_a_exp_mask_cap_kernel(tc, qT, kT, t, v, mask, out):
         def sbuf(name, shape, dtype):
             return sb.tile(shape, dtype, name=name, align_bytes=64)
 
-        q_raw = [sbuf("q_raw%d" % a, [P, PACK, NQ], F32) for a in range(2)]
-        q_bf = sbuf("q_bf", [P, 2 * NQ, PACK], BF16)
-        q_codes = sbuf("q_codes", [P, 2 * NQ], U32)
-        q_scales = sbuf("q_scales", [P, 2 * NQ], U8)
-
+        q_raw = {}
+        m_raw = {}
+        q_bf = sbuf("q_bf", [P, UNITS * QT, PACK], BF16)
+        q_codes = sbuf("q_codes", [P, UNITS * QT], U32)
+        q_scales = sbuf("q_scales", [P, UNITS * QT], U8)
         k_raw = sbuf("k_raw", [P, PACK, N], F32)
         k_bf = sbuf("k_bf", [P, PACK, P, PACK], BF16)
         k_codes = sbuf("k_codes", [P, PACK, P], U32)
         k_scales = sbuf("k_scales", [P, PACK, P], U8)
         t_sb = sbuf("t_sb", [P, PACK], F32)
-        m_raw = sbuf("m_raw", [P, PACK, NQ], F32)
-        mt = sbuf("mt", [P, PACK, NQ], F32)
+        mt = [sbuf("mt%d" % j, [P, PACK, 2 * QT], F32) for j in range(2)]
         v_raw = sbuf("v_raw", [P, KV, PACK, E], F32)
         v_bf = sbuf("v_bf", [P, KV, E, PACK], BF16)
         v_codes = sbuf("v_codes", [P, KV * E], U32)
         v_scales = sbuf("v_scales", [P, KV * E], U8)
-        th = [sbuf("th%d" % u, [P, KV, QT * PACK], F32) for u in range(8)]
-        pr = [sbuf("pr%d" % u, [P, KV, QT * PACK], F32) for u in range(8)]
-        w_bf = [sbuf("w_bf%d" % u, [P, KV, QT * PACK], BF16) for u in range(8)]
-        w_codes = [sbuf("w_codes%d" % u, [P, KV, QT], U32) for u in range(8)]
-        w_scales = [sbuf("w_scales%d" % u, [P, KV, QT], U8) for u in range(8)]
-        warm = sbuf("warm", [P, 2], F32)
+        th = [sbuf("th%d" % h, [P, PACK, QT], F32) for h in range(JOBS)]
+        pr = [sbuf("pr%d" % h, [P, PACK, QT], F32) for h in range(JOBS)]
+        w_bf = sbuf("w_bf", [P, JOBS * QT * PACK], BF16)
+        w_codes = sbuf("w_codes", [P, JOBS * QT], U32)
+        w_scales = sbuf("w_scales", [P, JOBS * QT], U8)
 
-        place = {ug: (gi, i) for gi, members in enumerate(GROUPS) for i, ug in enumerate(members)}
+        place = {h: (gi, i) for gi, members in enumerate(GROUPS) for i, h in enumerate(members)}
         recip = [sbuf("recip%d" % gi, [P, len(members)], F32) for gi, members in enumerate(GROUPS)]
         res = [sbuf("res%d" % gi, [P, len(members), E], F32) for gi, members in enumerate(GROUPS)]
         s_bank = {}
@@ -73,24 +65,28 @@ def tile_rows_a_exp_mask_cap_kernel(tc, qT, kT, t, v, mask, out):
         k_view = kT.rearrange("g (p j) n -> (g p) j n", j=PACK)
         m_view = mask.rearrange("(p r) q -> p r q", r=PACK)
 
-        def load_q(a, j, n):
-            cols = slice(j * QT, (j + n) * QT)
-            lo, hi = PAIRS[a]
+        def load_q(u, n):
+            raw = sbuf("q_raw%d" % u, [P, PACK, n * QT], F32)
+            for x in range(n):
+                q_raw[u + x] = (raw, x)
+            cols = slice((u % 4) * QT, (u % 4 + n) * QT)
+            lo, hi = PAIRS[u // 4]
             if hi == lo + 1:
                 rows = q_flat[lo * D : (hi + 1) * D, cols].rearrange("(p j) q -> p j q", j=PACK)
-                nc.sync.dma_start(out=q_raw[a][:, :, cols], in_=rows)
+                nc.sync.dma_start(out=raw[:], in_=rows)
             else:
-                for g, h in enumerate(PAIRS[a]):
-                    rows = qT[h, :, cols].rearrange("(p j) q -> p j q", j=PACK)
-                    nc.sync.dma_start(out=q_raw[a][g * ROWS : (g + 1) * ROWS, :, cols], in_=rows)
+                for g, head in enumerate(PAIRS[u // 4]):
+                    rows = qT[head, :, cols].rearrange("(p j) q -> p j q", j=PACK)
+                    nc.sync.dma_start(out=raw[g * ROWS : (g + 1) * ROWS], in_=rows)
 
-        def load_k(c):
-            cols = slice(PACK * K_CHUNKS[c][0], PACK * K_CHUNKS[c][1])
-            nc.sync.dma_start(out=k_raw[:, :, cols], in_=k_view[:, :, cols])
+        def load_k():
+            nc.sync.dma_start(out=k_raw[:], in_=k_view)
 
         def load_m(j, n):
-            cols = slice(j * QT, (j + n) * QT)
-            nc.sync.dma_start(out=m_raw[:, :, cols], in_=m_view[:, :, cols])
+            raw = sbuf("m_raw%d" % j, [P, PACK, n * QT], F32)
+            for x in range(n):
+                m_raw[j + x] = (raw, x)
+            nc.sync.dma_start(out=raw[:], in_=m_view[:, :, j * QT : (j + n) * QT])
 
         def load_v():
             nc.sync.dma_start(
@@ -98,13 +94,15 @@ def tile_rows_a_exp_mask_cap_kernel(tc, qT, kT, t, v, mask, out):
                 in_=v.rearrange("g (p r) e -> p g (r e)", r=PACK),
             )
 
-        def copy_q(u, n, on_scalar=False):
-            dst = q_bf[:, u * QT : (u + n) * QT, :].rearrange("p (c i) j -> p c j i", i=4)
-            src = q_raw[u // 4][:, :, (u % 4) * QT : (u % 4 + n) * QT].rearrange("p j (c i) -> p c j i", i=4)
-            if on_scalar:
-                nc.scalar.copy(out=dst, in_=src)
-            else:
-                nc.vector.tensor_copy(out=dst, in_=src)
+        def load_t():
+            nc.scalar.dma_start(out=t_sb[:], in_=t.rearrange("(p r) o -> p (r o)", r=PACK))
+
+        def copy_q(u, n):
+            raw, x = q_raw[u]
+            nc.vector.tensor_copy(
+                out=q_bf[:, u * QT : (u + n) * QT, :].rearrange("p (c i) j -> p c j i", i=4),
+                in_=raw[:, :, x * QT : (x + n) * QT].rearrange("p j (c i) -> p c j i", i=4),
+            )
 
         def quant_q(u, n):
             cols = slice(u * QT, (u + n) * QT)
@@ -114,40 +112,38 @@ def tile_rows_a_exp_mask_cap_kernel(tc, qT, kT, t, v, mask, out):
                 in_=q_bf[:, cols, :].rearrange("p q j -> p (q j)"),
             )
 
-        def copy_k(c, s0, s1, on_scalar=False):
-            dst = k_bf[:, :, s0:s1, :].rearrange("p r s j -> p s r j")
-            src = k_raw[:, :, PACK * s0 : PACK * s1].rearrange("p j (s r) -> p s r j", r=PACK)
+        def copy_k(r0, s0, s1, on_scalar=False):
+            dst = k_bf[:, r0 : r0 + 2, s0:s1, :].rearrange("p r s j -> p s j r")
+            src = k_raw[:].rearrange("p j (s r) -> p s j r", r=PACK)[:, s0:s1, :, r0 : r0 + 2]
             if on_scalar:
                 nc.scalar.copy(out=dst, in_=src)
             else:
                 nc.vector.tensor_copy(out=dst, in_=src)
 
-        def quant_k(hf):
-            cols = slice(64 * hf, 64 * hf + 64)
-            for r in range(PACK):
+        def quant_k(r0):
+            for r in (r0, r0 + 1):
                 nc.vector.quantize_mx(
-                    out=k_codes[:, r, cols].bitcast(FP8X4),
-                    scales=k_scales[:, r, cols],
-                    in_=k_bf[:, r, cols, :].rearrange("p s j -> p (s j)"),
+                    out=k_codes[:, r, :].bitcast(FP8X4),
+                    scales=k_scales[:, r, :],
+                    in_=k_bf[:, r].rearrange("p s j -> p (s j)"),
                 )
 
         def make_mt(j, n):
-            cols = slice(j * QT, (j + n) * QT)
+            raw, x = m_raw[j]
             for r in range(PACK):
                 nc.vector.tensor_scalar(
-                    out=mt[:, r, cols],
-                    in0=m_raw[:, r, cols],
+                    out=mt[j // 2][:, r, (j % 2) * QT : (j % 2 + n) * QT],
+                    in0=raw[:, r, x * QT : (x + n) * QT],
                     scalar1=t_sb[:, r : r + 1],
                     scalar2=None,
                     op0=ALU.mult,
                 )
 
-        def copy_v():
-            for g in range(KV):
-                nc.vector.tensor_copy(
-                    out=v_bf[:, g].rearrange("p (c i) r -> p c r i", i=4),
-                    in_=v_raw[:, g].rearrange("p r (c i) -> p c r i", i=4),
-                )
+        def copy_v(g):
+            nc.vector.tensor_copy(
+                out=v_bf[:, g].rearrange("p (c i) r -> p c r i", i=4),
+                in_=v_raw[:, g].rearrange("p r (c i) -> p c r i", i=4),
+            )
 
         def quant_v():
             nc.vector.quantize_mx(
@@ -156,121 +152,82 @@ def tile_rows_a_exp_mask_cap_kernel(tc, qT, kT, t, v, mask, out):
                 in_=v_bf[:].rearrange("p g e r -> p (g e r)"),
             )
 
-        def scores(u):
+        def scores(h):
+            u, g = divmod(h, KV)
             cols = slice(u * QT, (u + 1) * QT)
-            for g in range(KV):
-                s_bank[u, g] = ps.tile([P, PACK, QT], F32, name="s%d_%d" % (u, g), tag="s%d_%d" % (g, u % 2))
+            rows = slice(g * ROWS, (g + 1) * ROWS)
+            s_bank[h] = ps.tile([P, PACK, QT], F32, name="s%d" % h, tag="s%d" % (h % 4))
             for r in range(PACK):
-                for g in range(KV):
-                    rows = slice(g * ROWS, (g + 1) * ROWS)
-                    nc.tensor.matmul_mx(
-                        out=s_bank[u, g][:, r, :],
-                        lhsT=k_codes[rows, r, :].bitcast(FP8X4),
-                        lhsT_scale=k_scales[rows, r, :],
-                        rhs=q_codes[rows, cols].bitcast(FP8X4),
-                        rhs_scale=q_scales[rows, cols],
-                        start=True,
-                        stop=True,
-                    )
-
-        def cap(u, g):
-            nc.scalar.activation(
-                out=th[u][:, g, :],
-                in_=s_bank[u, g][:].rearrange("p r q -> p (r q)"),
-                func=ACT.Tanh,
-                scale=1.0 / CAP,
-            )
-
-        def heads(g):
-            return slice(0, KV) if g is None else slice(g, g + 1)
-
-        def expo(u, g=None):
-            gs = heads(g)
-            nc.scalar.activation(out=pr[u][:, gs, :], in_=th[u][:, gs, :], func=ACT.Exp, scale=CAP)
-
-        def weigh(u, g=None):
-            gs = heads(g)
-            j = u % 4
-            m = mt[:, :, j * QT : (j + 1) * QT].rearrange("p r (c i) -> p c r i", i=2)
-            for x in range(gs.start, gs.stop):
-                nc.vector.tensor_tensor(
-                    out=w_bf[u][:, x, :].rearrange("p (c i r) -> p c r i", i=2, r=PACK),
-                    in0=pr[u][:, x, :].rearrange("p (r c i) -> p c r i", i=2, r=PACK),
-                    in1=m,
-                    op=ALU.mult,
-                )
-
-        def expo_half(u, g, hf):
-            cols = slice(hf * QT // 2, (hf + 1) * QT // 2)
-            nc.scalar.activation(
-                out=pr[u][:, g, :].rearrange("p (r q) -> p r q", r=PACK)[:, :, cols],
-                in_=th[u][:, g, :].rearrange("p (r q) -> p r q", r=PACK)[:, :, cols],
-                func=ACT.Exp,
-                scale=CAP,
-            )
-
-        def weigh_half(u, g, hf):
-            j = u % 4
-            pairs = slice(hf * QT // 4, (hf + 1) * QT // 4)
-            m = mt[:, :, j * QT : (j + 1) * QT].rearrange("p r (c i) -> p c r i", i=2)
-            nc.vector.tensor_tensor(
-                out=w_bf[u][:, g, :].rearrange("p (c i r) -> p c r i", i=2, r=PACK)[:, pairs],
-                in0=pr[u][:, g, :].rearrange("p (r c i) -> p c r i", i=2, r=PACK)[:, pairs],
-                in1=m[:, pairs],
-                op=ALU.mult,
-            )
-
-        def quant_w(u, g=None):
-            gs = heads(g)
-            nc.vector.quantize_mx(
-                out=w_codes[u][:, gs, :].rearrange("p g q -> p (g q)").bitcast(FP8X4),
-                scales=w_scales[u][:, gs, :].rearrange("p g q -> p (g q)"),
-                in_=w_bf[u][:, gs, :].rearrange("p g x -> p (g x)"),
-            )
-
-        def second(u, g=None):
-            gs = heads(g)
-            for x in range(gs.start, gs.stop):
-                gi, i = place[u, x]
-                if gi not in y_bank:
-                    y_bank[gi] = ps.tile([P, 2 * KV, E], F32, name="y%d" % gi, tag="y%d" % (gi % 4))
-                cols = slice(x * E, (x + 1) * E)
                 nc.tensor.matmul_mx(
-                    out=y_bank[gi][:, i, :],
-                    lhsT=w_codes[u][:, x, :].bitcast(FP8X4),
-                    lhsT_scale=w_scales[u][:, x, :],
-                    rhs=v_codes[:, cols].bitcast(FP8X4),
-                    rhs_scale=v_scales[:, cols],
+                    out=s_bank[h][:, r, :],
+                    lhsT=k_codes[rows, r, :].bitcast(FP8X4),
+                    lhsT_scale=k_scales[rows, r, :],
+                    rhs=q_codes[rows, cols].bitcast(FP8X4),
+                    rhs_scale=q_scales[rows, cols],
                     start=True,
                     stop=True,
                 )
+
+        def cap(h, q0=0, q1=QT):
+            nc.scalar.activation(out=th[h][:, :, q0:q1], in_=s_bank[h][:, :, q0:q1], func=ACT.Tanh, scale=1.0 / CAP)
+
+        def expo(h, q0=0, q1=QT):
+            nc.scalar.activation(out=pr[h][:, :, q0:q1], in_=th[h][:, :, q0:q1], func=ACT.Exp, scale=CAP)
+
+        def weigh(h, q0=0, q1=QT):
+            j = (h // KV) % 4
+            first = (j % 2) * QT
+            nc.vector.tensor_tensor(
+                out=w_bf[:, (h * QT + q0) * PACK : (h * QT + q1) * PACK].rearrange("p (c i r) -> p c r i", i=2, r=PACK),
+                in0=pr[h][:, :, q0:q1].rearrange("p r (c i) -> p c r i", i=2),
+                in1=mt[j // 2][:, :, first + q0 : first + q1].rearrange("p r (c i) -> p c r i", i=2),
+                op=ALU.mult,
+            )
+
+        def quant_w(h, n=1):
+            nc.vector.quantize_mx(
+                out=w_codes[:, h * QT : (h + n) * QT].bitcast(FP8X4),
+                scales=w_scales[:, h * QT : (h + n) * QT],
+                in_=w_bf[:, h * QT * PACK : (h + n) * QT * PACK],
+            )
+
+        def second(h):
+            gi, i = place[h]
+            if gi not in y_bank:
+                y_bank[gi] = ps.tile([P, 2 * KV, E], F32, name="y%d" % gi, tag="y%d" % (gi % 4))
+            cols = slice((h % KV) * E, (h % KV + 1) * E)
+            nc.tensor.matmul_mx(
+                out=y_bank[gi][:, i, :],
+                lhsT=w_codes[:, h * QT : (h + 1) * QT].bitcast(FP8X4),
+                lhsT_scale=w_scales[:, h * QT : (h + 1) * QT],
+                rhs=v_codes[:, cols].bitcast(FP8X4),
+                rhs_scale=v_scales[:, cols],
+                start=True,
+                stop=True,
+            )
 
         def invert(gi):
             n = len(GROUPS[gi])
             nc.vector.reciprocal(out=recip[gi][:], in_=y_bank[gi][:, 0:n, E - 1])
 
-        def divide(gi, on_scalar=False):
-            n = len(GROUPS[gi])
+        def divide(gi, i0, n, on_scalar=False):
             if on_scalar:
-                for x in range(n):
+                for x in range(i0, i0 + n):
                     nc.scalar.activation(
                         out=res[gi][:, x, :], in_=y_bank[gi][:, x, :], func=ACT.Copy, scale=recip[gi][:, x : x + 1]
                     )
             else:
                 nc.vector.tensor_tensor(
-                    out=res[gi][:],
-                    in0=y_bank[gi][:, 0:n, :],
-                    in1=recip[gi][:].unsqueeze(2).to_broadcast([P, n, E]),
+                    out=res[gi][:, i0 : i0 + n, :],
+                    in0=y_bank[gi][:, i0 : i0 + n, :],
+                    in1=recip[gi][:, i0 : i0 + n].unsqueeze(2).to_broadcast([P, n, E]),
                     op=ALU.mult,
                 )
-
-        def store(gi):
-            members = GROUPS[gi]
-            for i in range(0, len(members), KV):
-                u, g = members[i]
+            for i in range(i0, i0 + n, KV):
+                u, g = divmod(GROUPS[gi][i], KV)
                 rows = slice((u % 4) * QT, (u % 4 + 1) * QT)
                 lo, hi = PAIRS[u // 4]
-                if len(members) == 1:
+                if n == 1:
                     nc.sync.dma_start(out=out[PAIRS[u // 4][g], rows, :], in_=res[gi][:, 0, :])
                 else:
                     nc.sync.dma_start(
@@ -278,122 +235,87 @@ def tile_rows_a_exp_mask_cap_kernel(tc, qT, kT, t, v, mask, out):
                         in_=res[gi][:, i : i + KV, :],
                     )
 
-        def load_t():
-            nc.scalar.dma_start(out=t_sb[:], in_=t.rearrange("(p r) o -> p (r o)", r=PACK))
-
-        def warm_up():
-            nc.vector.memset(warm[:, 0:1], 0.0)
-            nc.scalar.activation(out=warm[:, 1:2], in_=warm[:, 0:1], func=ACT.Exp)
-
-        load_k(0)
-        load_q(0, 0, 1)
-        load_k(1)
-        load_q(0, 1, 1)
-        load_q(0, 2, 2)
-        load_m(0, 2)
-        load_v()
-        load_q(1, 0, 2)
-        load_m(2, 2)
-        load_q(1, 2, 2)
         load_t()
-        warm_up()
-        copy_k(0, 0, 64)
-        copy_k(0, 64, 96, on_scalar=True)
+        load_k()
+        load_q(0, 1)
+        load_q(1, 2)
+        load_m(0, 2)
+        load_q(3, 1)
+        load_v()
+        load_q(4, 1)
+        load_m(2, 2)
+        for u in range(5, UNITS):
+            load_q(u, 1)
+
+        copy_k(0, 0, P)
+        copy_k(2, K_SPLIT, P, on_scalar=True)
+        copy_k(2, 0, K_SPLIT)
         copy_q(0, 1)
         quant_k(0)
         quant_q(0, 1)
-        copy_k(1, 96, K_SPLIT)
-        copy_k(1, K_SPLIT, 128, on_scalar=True)
-        quant_k(1)
+        quant_k(2)
         scores(0)
-        cap(0, 0)
-        copy_q(1, 1)
-        quant_q(1, 1)
         scores(1)
-        copy_q(2, 2)
-        cap(0, 1)
-        cap(1, 0)
-        quant_q(2, 2)
+        copy_q(1, 1)
+        copy_q(2, 1)
+        quant_q(1, 1)
         scores(2)
-        make_mt(0, 2)
-        expo(0)
-        cap(1, 1)
-        weigh(0)
-        copy_v()
-        cap(2, 0)
-        expo(1)
-        cap(2, 1)
         scores(3)
-        quant_w(0)
-        weigh(1)
-        cap(3, 0)
-        copy_q(4, 2)
-        cap(3, 1)
-        quant_w(1)
-        quant_q(4, 2)
-        make_mt(2, 2)
-        expo(2)
-        quant_v()
-        scores(4)
-        expo(3)
-        cap(4, 0)
-        cap(4, 1)
-        weigh(2)
-        weigh(3)
-        copy_q(6, 2)
-        quant_w(2)
-        scores(5)
-        second(0)
-        cap(5, 0)
-        cap(5, 1)
-        second(1)
-        quant_q(6, 2)
-        scores(6)
-        invert(0)
-        expo(4)
-        quant_w(3)
-        weigh(4)
-        expo(5)
-        cap(6, 0)
-        scores(7)
-        weigh(5)
-        quant_w(4)
-        cap(6, 1)
-        quant_w(5)
-        second(2)
-        cap(7, 0)
-        second(3)
-        invert(1)
-        divide(0)
-        expo(6)
-        cap(7, 1)
-        second(4)
-        second(5)
-        expo(7, 0)
-        store(0)
-        expo_half(7, 1, 0)
-        weigh(6)
-        divide(1, on_scalar=True)
-        invert(2)
-        weigh(7, 0)
-        quant_w(6)
-        second(6)
-        store(1)
-        expo_half(7, 1, 1)
-        weigh_half(7, 1, 0)
-        weigh_half(7, 1, 1)
-        quant_w(7, 0)
+        quant_q(2, 1)
+        make_mt(0, 2)
+        copy_q(3, 1)
+
+        chores = {
+            0: [lambda: copy_v(0)],
+            2: [lambda: copy_v(1)],
+            3: [lambda: make_mt(2, 2)],
+            4: [quant_v],
+            8: [lambda: invert(0)],
+            9: [lambda: divide(0, 0, 4)],
+            10: [lambda: invert(1)],
+            11: [lambda: divide(1, 0, 2)],
+            13: [lambda: invert(2)],
+        }
+        cap(0)
+        done = 0
+        last = JOBS - 1
+        for h in range(last - 1):
+            cap(h + 1)
+            expo(h)
+            weigh(h)
+            if h > 0:
+                quant_w(h - 1)
+            for chore in chores.get(h, []):
+                chore()
+            u = (h + 1) // 2 + 3
+            if u < UNITS:
+                (copy_q if h % 2 else quant_q)(u, 1)
+            if h + 4 < JOBS:
+                scores(h + 4)
+            if h >= 5:
+                upto = h - 1 if h + 4 < JOBS else h
+                for x in range(done, upto):
+                    second(x)
+                done = upto
+        cap(last, 0, QT // 2)
+        expo(last - 1)
+        cap(last, QT // 2, QT)
+        expo(last, 0, QT // 2)
+        expo(last, QT // 2, QT)
+        divide(1, 2, 2, on_scalar=True)
+        divide(2, 0, 4, on_scalar=True)
+        weigh(last - 1)
+        quant_w(last - 2)
+        second(last - 2)
+        weigh(last, 0, QT // 2)
+        weigh(last, QT // 2, QT)
+        quant_w(last - 1)
+        second(last - 1)
         invert(3)
-        second(7, 0)
-        divide(2, on_scalar=True)
-        store(2)
-        quant_w(7, 1)
-        second(7, 1)
+        quant_w(last)
+        second(last)
+        divide(3, 0, 2, on_scalar=True)
         invert(4)
-        divide(3, on_scalar=True)
         invert(5)
-        store(3)
-        divide(4)
-        store(4)
-        divide(5)
-        store(5)
+        divide(4, 0, 1, on_scalar=True)
+        divide(5, 0, 1)

@@ -20,7 +20,7 @@ FLOPS = 2 * H * N * NQ * D + 2 * H * NQ * N * E
 PAIRS = ((1, 2), (0, 3))
 UNITS = 8
 JOBS = 2 * UNITS
-K_SPLIT = 40
+QUAD = 32
 GROUPS = ((0, 1, 2, 3), (4, 5, 6, 7), (8, 9, 10, 11), (12, 13), (14,), (15,))
 
 
@@ -43,7 +43,9 @@ def tile_rows_a_exp_mask_cap_kernel(tc, qT, kT, t, v, mask, out):
         k_bf = sbuf("k_bf", [P, PACK, P, PACK], BF16)
         k_codes = sbuf("k_codes", [P, PACK, P], U32)
         k_scales = sbuf("k_scales", [P, PACK, P], U8)
-        t_sb = sbuf("t_sb", [P, PACK], F32)
+        t_rows = sbuf("t_rows", [P, P], F32)
+        t_dealt = sbuf("t_dealt", [P, P], F32)
+        t_sb = sbuf("t_sb", [P, P], F32)
         mt = [sbuf("mt%d" % j, [P, PACK, 2 * QT], F32) for j in range(2)]
         v_raw = sbuf("v_raw", [P, KV, PACK, E], F32)
         v_bf = sbuf("v_bf", [P, KV, E, PACK], BF16)
@@ -59,6 +61,7 @@ def tile_rows_a_exp_mask_cap_kernel(tc, qT, kT, t, v, mask, out):
         recip = [sbuf("recip%d" % gi, [P, len(members)], F32) for gi, members in enumerate(GROUPS)]
         res = [sbuf("res%d" % gi, [P, len(members), E], F32) for gi, members in enumerate(GROUPS)]
         s_bank = {}
+        turn = [1, 1]
         y_bank = {}
 
         q_flat = qT.rearrange("h d q -> (h d) q")
@@ -95,7 +98,16 @@ def tile_rows_a_exp_mask_cap_kernel(tc, qT, kT, t, v, mask, out):
             )
 
         def load_t():
-            nc.scalar.dma_start(out=t_sb[:], in_=t.rearrange("(p r) o -> p (r o)", r=PACK))
+            nc.sync.dma_start(out=t_rows[0:P:QUAD, :], in_=t.rearrange("(g n) o -> g (n o)", n=P))
+
+        def turn_t():
+            nc.vector.memset(t_dealt[:], 0.0)
+            for p in range(0, P, QUAD):
+                nc.vector.tensor_copy(
+                    out=t_dealt[p : p + 1].rearrange("p (r a) -> p r a", r=PACK),
+                    in_=t_rows[p : p + 1].rearrange("p (a r) -> p r a", r=PACK),
+                )
+            nc.vector.transpose(out=t_sb[:], in_=t_dealt[:])
 
         def copy_q(u, n):
             raw, x = q_raw[u]
@@ -120,13 +132,12 @@ def tile_rows_a_exp_mask_cap_kernel(tc, qT, kT, t, v, mask, out):
             else:
                 nc.vector.tensor_copy(out=dst, in_=src)
 
-        def quant_k(r0):
-            for r in (r0, r0 + 1):
-                nc.vector.quantize_mx(
-                    out=k_codes[:, r, :].bitcast(FP8X4),
-                    scales=k_scales[:, r, :],
-                    in_=k_bf[:, r].rearrange("p s j -> p (s j)"),
-                )
+        def quant_k(r):
+            nc.vector.quantize_mx(
+                out=k_codes[:, r, :].bitcast(FP8X4),
+                scales=k_scales[:, r, :],
+                in_=k_bf[:, r].rearrange("p s j -> p (s j)"),
+            )
 
         def make_mt(j, n):
             raw, x = m_raw[j]
@@ -134,15 +145,15 @@ def tile_rows_a_exp_mask_cap_kernel(tc, qT, kT, t, v, mask, out):
                 nc.vector.tensor_scalar(
                     out=mt[j // 2][:, r, (j % 2) * QT : (j % 2 + n) * QT],
                     in0=raw[:, r, x * QT : (x + n) * QT],
-                    scalar1=t_sb[:, r : r + 1],
+                    scalar1=t_sb[:, r * QUAD : r * QUAD + 1],
                     scalar2=None,
                     op0=ALU.mult,
                 )
 
-        def copy_v(g):
+        def copy_v():
             nc.vector.tensor_copy(
-                out=v_bf[:, g].rearrange("p (c i) r -> p c r i", i=4),
-                in_=v_raw[:, g].rearrange("p r (c i) -> p c r i", i=4),
+                out=v_bf[:].rearrange("p g (c i) r -> p g c r i", i=4),
+                in_=v_raw[:].rearrange("p g r (c i) -> p g c r i", i=4),
             )
 
         def quant_v():
@@ -152,14 +163,15 @@ def tile_rows_a_exp_mask_cap_kernel(tc, qT, kT, t, v, mask, out):
                 in_=v_bf[:].rearrange("p g e r -> p (g e r)"),
             )
 
-        def scores(h):
+        def scores(h, r0=0, r1=PACK):
             u, g = divmod(h, KV)
             cols = slice(u * QT, (u + 1) * QT)
             rows = slice(g * ROWS, (g + 1) * ROWS)
-            s_bank[h] = ps.tile([P, PACK, QT], F32, name="s%d" % h, tag="s%d" % (h % 4))
-            for r in range(PACK):
+            turn[g] = 1 - turn[g]
+            s_bank[h, r0] = ps.tile([P, PACK, QT], F32, name="s%d_%d" % (h, r0), tag="s%d%d" % (g, turn[g]))
+            for r in range(r0, r1):
                 nc.tensor.matmul_mx(
-                    out=s_bank[h][:, r, :],
+                    out=s_bank[h, r0][:, r, :],
                     lhsT=k_codes[rows, r, :].bitcast(FP8X4),
                     lhsT_scale=k_scales[rows, r, :],
                     rhs=q_codes[rows, cols].bitcast(FP8X4),
@@ -168,11 +180,13 @@ def tile_rows_a_exp_mask_cap_kernel(tc, qT, kT, t, v, mask, out):
                     stop=True,
                 )
 
-        def cap(h, q0=0, q1=QT):
-            nc.scalar.activation(out=th[h][:, :, q0:q1], in_=s_bank[h][:, :, q0:q1], func=ACT.Tanh, scale=1.0 / CAP)
+        def cap(h, q0=0, q1=QT, r0=0, r1=PACK):
+            nc.scalar.activation(
+                out=th[h][:, r0:r1, q0:q1], in_=s_bank[h, r0][:, r0:r1, q0:q1], func=ACT.Tanh, scale=1.0 / CAP
+            )
 
-        def expo(h, q0=0, q1=QT):
-            nc.scalar.activation(out=pr[h][:, :, q0:q1], in_=th[h][:, :, q0:q1], func=ACT.Exp, scale=CAP)
+        def expo(h, q0=0, q1=QT, r0=0, r1=PACK):
+            nc.scalar.activation(out=pr[h][:, r0:r1, q0:q1], in_=th[h][:, r0:r1, q0:q1], func=ACT.Exp, scale=CAP)
 
         def weigh(h, q0=0, q1=QT):
             j = (h // KV) % 4
@@ -184,11 +198,11 @@ def tile_rows_a_exp_mask_cap_kernel(tc, qT, kT, t, v, mask, out):
                 op=ALU.mult,
             )
 
-        def quant_w(h, n=1):
+        def quant_w(h, q0=0, q1=QT):
             nc.vector.quantize_mx(
-                out=w_codes[:, h * QT : (h + n) * QT].bitcast(FP8X4),
-                scales=w_scales[:, h * QT : (h + n) * QT],
-                in_=w_bf[:, h * QT * PACK : (h + n) * QT * PACK],
+                out=w_codes[:, h * QT + q0 : h * QT + q1].bitcast(FP8X4),
+                scales=w_scales[:, h * QT + q0 : h * QT + q1],
+                in_=w_bf[:, (h * QT + q0) * PACK : (h * QT + q1) * PACK],
             )
 
         def second(h):
@@ -247,15 +261,21 @@ def tile_rows_a_exp_mask_cap_kernel(tc, qT, kT, t, v, mask, out):
         for u in range(5, UNITS):
             load_q(u, 1)
 
+        turn_t()
         copy_k(0, 0, P)
-        copy_k(2, K_SPLIT, P, on_scalar=True)
-        copy_k(2, 0, K_SPLIT)
+        copy_k(2, 0, P, on_scalar=True)
         copy_q(0, 1)
         quant_k(0)
+        quant_k(1)
         quant_q(0, 1)
         quant_k(2)
-        scores(0)
+        quant_k(3)
+        scores(0, 0, 2)
+        scores(0, 2, PACK)
         scores(1)
+        cap(0, r1=2)
+        cap(0, r0=2)
+        expo(0, r1=2)
         copy_q(1, 1)
         copy_q(2, 1)
         quant_q(1, 1)
@@ -266,30 +286,30 @@ def tile_rows_a_exp_mask_cap_kernel(tc, qT, kT, t, v, mask, out):
         copy_q(3, 1)
 
         chores = {
-            0: [lambda: copy_v(0)],
-            2: [lambda: copy_v(1)],
-            3: [lambda: make_mt(2, 2)],
-            4: [quant_v],
+            0: [lambda: quant_q(3, 1)],
+            1: [copy_v],
+            3: [lambda: make_mt(2, 2), quant_v],
             8: [lambda: invert(0)],
-            9: [lambda: divide(0, 0, 4)],
-            10: [lambda: invert(1)],
+            9: [lambda: divide(0, 0, 2)],
+            10: [lambda: divide(0, 2, 2), lambda: invert(1)],
             11: [lambda: divide(1, 0, 2)],
-            13: [lambda: invert(2)],
+            12: [lambda: divide(1, 2, 2)],
         }
-        cap(0)
         done = 0
         last = JOBS - 1
         for h in range(last - 1):
             cap(h + 1)
-            expo(h)
-            weigh(h)
-            if h > 0:
+            expo(h, r0=2 if h == 0 else 0)
+            if h == last - 2:
                 quant_w(h - 1)
+            weigh(h)
+            if 0 < h < last - 2:
+                quant_w(h - 1)
+            u = h // 2 + 3
+            if 3 < u < UNITS:
+                (quant_q if h % 2 else copy_q)(u, 1)
             for chore in chores.get(h, []):
                 chore()
-            u = (h + 1) // 2 + 3
-            if u < UNITS:
-                (copy_q if h % 2 else quant_q)(u, 1)
             if h + 4 < JOBS:
                 scores(h + 4)
             if h >= 5:
@@ -297,22 +317,26 @@ def tile_rows_a_exp_mask_cap_kernel(tc, qT, kT, t, v, mask, out):
                 for x in range(done, upto):
                     second(x)
                 done = upto
-        cap(last, 0, QT // 2)
+        half, quarter = QT // 2, QT // 4
         expo(last - 1)
-        cap(last, QT // 2, QT)
-        expo(last, 0, QT // 2)
-        expo(last, QT // 2, QT)
-        divide(1, 2, 2, on_scalar=True)
-        divide(2, 0, 4, on_scalar=True)
+        cap(last, 0, half)
+        cap(last, half, QT)
+        expo(last, 0, half)
+        expo(last, half, QT - quarter)
+        expo(last, QT - quarter, QT)
         weigh(last - 1)
         quant_w(last - 2)
         second(last - 2)
-        weigh(last, 0, QT // 2)
-        weigh(last, QT // 2, QT)
+        invert(2)
+        divide(2, 0, 4, on_scalar=True)
         quant_w(last - 1)
         second(last - 1)
+        weigh(last, 0, half)
+        weigh(last, half, QT - quarter)
+        weigh(last, QT - quarter, QT)
+        quant_w(last, 0, half)
         invert(3)
-        quant_w(last)
+        quant_w(last, half, QT)
         second(last)
         divide(3, 0, 2, on_scalar=True)
         invert(4)

@@ -21,6 +21,7 @@ PAIRS = ((1, 2), (0, 3))
 UNITS = 8
 JOBS = 2 * UNITS
 QUAD = 32
+PAIRED = 10
 GROUPS = ((0, 1, 2, 3), (4, 5, 6, 7), (8, 9, 10, 11), (12, 13), (14,), (15,))
 
 
@@ -98,15 +99,16 @@ def tile_rows_a_exp_mask_cap_kernel(tc, qT, kT, t, v, mask, out):
             )
 
         def load_t():
+            nc.vector.memset(t_rows[:], 0.0)
             nc.sync.dma_start(out=t_rows[0:P:QUAD, :], in_=t.rearrange("(g n) o -> g (n o)", n=P))
 
+        def deal_t():
+            nc.vector.tensor_copy(
+                out=t_dealt[:].rearrange("p (r a) -> p r a", r=PACK),
+                in_=t_rows[:].rearrange("p (a r) -> p r a", r=PACK),
+            )
+
         def turn_t():
-            nc.vector.memset(t_dealt[:], 0.0)
-            for p in range(0, P, QUAD):
-                nc.vector.tensor_copy(
-                    out=t_dealt[p : p + 1].rearrange("p (r a) -> p r a", r=PACK),
-                    in_=t_rows[p : p + 1].rearrange("p (a r) -> p r a", r=PACK),
-                )
             nc.vector.transpose(out=t_sb[:], in_=t_dealt[:])
 
         def copy_q(u, n):
@@ -163,22 +165,30 @@ def tile_rows_a_exp_mask_cap_kernel(tc, qT, kT, t, v, mask, out):
                 in_=v_bf[:].rearrange("p g e r -> p (g e r)"),
             )
 
-        def scores(h, r0=0, r1=PACK):
-            u, g = divmod(h, KV)
-            cols = slice(u * QT, (u + 1) * QT)
-            rows = slice(g * ROWS, (g + 1) * ROWS)
+        def take_bank(h, r0=0):
+            g = h % KV
             turn[g] = 1 - turn[g]
             s_bank[h, r0] = ps.tile([P, PACK, QT], F32, name="s%d_%d" % (h, r0), tag="s%d%d" % (g, turn[g]))
-            for r in range(r0, r1):
-                nc.tensor.matmul_mx(
-                    out=s_bank[h, r0][:, r, :],
-                    lhsT=k_codes[rows, r, :].bitcast(FP8X4),
-                    lhsT_scale=k_scales[rows, r, :],
-                    rhs=q_codes[rows, cols].bitcast(FP8X4),
-                    rhs_scale=q_scales[rows, cols],
-                    start=True,
-                    stop=True,
-                )
+
+        def scores(u):
+            cols = slice(u * QT, (u + 1) * QT)
+            for g in range(KV):
+                take_bank(KV * u + g)
+            for r in range(PACK):
+                if u == 0 and r == 2:
+                    take_bank(0, 2)
+                for g in range(KV):
+                    h = KV * u + g
+                    rows = slice(g * ROWS, (g + 1) * ROWS)
+                    nc.tensor.matmul_mx(
+                        out=s_bank[h, 2 if h == 0 and r >= 2 else 0][:, r, :],
+                        lhsT=k_codes[rows, r, :].bitcast(FP8X4),
+                        lhsT_scale=k_scales[rows, r, :],
+                        rhs=q_codes[rows, cols].bitcast(FP8X4),
+                        rhs_scale=q_scales[rows, cols],
+                        start=True,
+                        stop=True,
+                    )
 
         def cap(h, q0=0, q1=QT, r0=0, r1=PACK):
             nc.scalar.activation(
@@ -249,8 +259,8 @@ def tile_rows_a_exp_mask_cap_kernel(tc, qT, kT, t, v, mask, out):
                         in_=res[gi][:, i : i + KV, :],
                     )
 
-        load_t()
         load_k()
+        load_t()
         load_q(0, 1)
         load_q(1, 2)
         load_m(0, 2)
@@ -261,85 +271,87 @@ def tile_rows_a_exp_mask_cap_kernel(tc, qT, kT, t, v, mask, out):
         for u in range(5, UNITS):
             load_q(u, 1)
 
-        turn_t()
         copy_k(0, 0, P)
+        deal_t()
         copy_k(2, 0, P, on_scalar=True)
         copy_q(0, 1)
         quant_k(0)
-        quant_k(1)
         quant_q(0, 1)
+        quant_k(1)
         quant_k(2)
         quant_k(3)
-        scores(0, 0, 2)
-        scores(0, 2, PACK)
-        scores(1)
+        turn_t()
+        scores(0)
         cap(0, r1=2)
         cap(0, r0=2)
         expo(0, r1=2)
         copy_q(1, 1)
         copy_q(2, 1)
         quant_q(1, 1)
-        scores(2)
-        scores(3)
+        scores(1)
         quant_q(2, 1)
         make_mt(0, 2)
         copy_q(3, 1)
 
         chores = {
-            0: [lambda: quant_q(3, 1)],
-            1: [copy_v],
+            0: [lambda: quant_q(3, 1), copy_v],
             3: [lambda: make_mt(2, 2), quant_v],
-            8: [lambda: invert(0)],
-            9: [lambda: divide(0, 0, 2)],
-            10: [lambda: divide(0, 2, 2), lambda: invert(1)],
-            11: [lambda: divide(1, 0, 2)],
-            12: [lambda: divide(1, 2, 2)],
+            6: [lambda: invert(0)],
+            7: [lambda: divide(0, 0, 2)],
+            9: [lambda: divide(0, 2, 2), lambda: invert(1)],
+            10: [lambda: divide(1, 0, 2)],
+            11: [lambda: divide(1, 2, 2)],
         }
         done = 0
         last = JOBS - 1
-        for h in range(last - 1):
+        for h in range(last - 2):
             cap(h + 1)
             expo(h, r0=2 if h == 0 else 0)
-            if h == last - 2:
-                quant_w(h - 1)
             weigh(h)
-            if 0 < h < last - 2:
+            if h > PAIRED:
                 quant_w(h - 1)
+            elif h > 0 and h % 2 == 0:
+                quant_w(h - 2, 0, 2 * QT)
             u = h // 2 + 3
             if 3 < u < UNITS:
                 (quant_q if h % 2 else copy_q)(u, 1)
             for chore in chores.get(h, []):
                 chore()
-            if h + 4 < JOBS:
-                scores(h + 4)
-            if h >= 5:
-                upto = h - 1 if h + 4 < JOBS else h
-                for x in range(done, upto):
+            if h % 2 == 0 and h + 4 < JOBS:
+                scores(h // 2 + 2)
+            if h > PAIRED or (h >= 4 and h % 2 == 0):
+                for x in range(done, h):
                     second(x)
-                done = upto
+                done = h
         half, quarter = QT // 2, QT // 4
-        expo(last - 1)
+        expo(last - 2)
+        cap(last - 1, 0, half)
+        cap(last - 1, half, QT)
+        expo(last - 1, 0, half)
+        expo(last - 1, half, QT)
         cap(last, 0, half)
         cap(last, half, QT)
-        expo(last, 0, half)
-        expo(last, half, QT - quarter)
-        expo(last, QT - quarter, QT)
-        weigh(last - 1)
+        for q0 in range(0, QT, quarter):
+            expo(last, q0, q0 + quarter)
+        weigh(last - 2)
+        quant_w(last - 3)
+        second(last - 3)
+        weigh(last - 1, 0, half)
         quant_w(last - 2)
         second(last - 2)
+        weigh(last - 1, half, QT)
         invert(2)
         divide(2, 0, 4, on_scalar=True)
         quant_w(last - 1)
         second(last - 1)
-        weigh(last, 0, half)
-        weigh(last, half, QT - quarter)
-        weigh(last, QT - quarter, QT)
-        quant_w(last, 0, half)
+        for q0 in range(0, QT, quarter):
+            weigh(last, q0, q0 + quarter)
         invert(3)
+        divide(3, 0, 2, on_scalar=True)
+        quant_w(last, 0, half)
         quant_w(last, half, QT)
         second(last)
-        divide(3, 0, 2, on_scalar=True)
         invert(4)
-        invert(5)
         divide(4, 0, 1, on_scalar=True)
+        invert(5)
         divide(5, 0, 1)

@@ -176,12 +176,13 @@ def tile_rows_a_exp_mask_cap_kernel(tc, qT, kT, t, v, mask, out):
                 take_bank(KV * u + g)
             for r in range(PACK):
                 if u == 0 and r == 2:
-                    take_bank(0, 2)
+                    for g in range(KV):
+                        take_bank(g, 2)
                 for g in range(KV):
                     h = KV * u + g
                     rows = slice(g * ROWS, (g + 1) * ROWS)
                     nc.tensor.matmul_mx(
-                        out=s_bank[h, 2 if h == 0 and r >= 2 else 0][:, r, :],
+                        out=s_bank[h, 2 if u == 0 and r >= 2 else 0][:, r, :],
                         lhsT=k_codes[rows, r, :].bitcast(FP8X4),
                         lhsT_scale=k_scales[rows, r, :],
                         rhs=q_codes[rows, cols].bitcast(FP8X4),
@@ -283,8 +284,11 @@ def tile_rows_a_exp_mask_cap_kernel(tc, qT, kT, t, v, mask, out):
         turn_t()
         scores(0)
         cap(0, r1=2)
+        cap(1, r1=2)
         cap(0, r0=2)
-        expo(0, r1=2)
+        cap(1, r0=2)
+        expo(0)
+        expo(1)
         copy_q(1, 1)
         copy_q(2, 1)
         quant_q(1, 1)
@@ -294,8 +298,10 @@ def tile_rows_a_exp_mask_cap_kernel(tc, qT, kT, t, v, mask, out):
         copy_q(3, 1)
 
         chores = {
-            0: [lambda: quant_q(3, 1), copy_v],
-            3: [lambda: make_mt(2, 2), quant_v],
+            0: [lambda: quant_q(3, 1)],
+            1: [copy_v, lambda: quant_w(0, 0, 2 * QT)],
+            2: [quant_v],
+            3: [lambda: make_mt(2, 2), lambda: quant_w(2, 0, 2 * QT)],
             6: [lambda: invert(0)],
             7: [lambda: divide(0, 0, 2)],
             9: [lambda: divide(0, 2, 2), lambda: invert(1)],
@@ -305,12 +311,14 @@ def tile_rows_a_exp_mask_cap_kernel(tc, qT, kT, t, v, mask, out):
         done = 0
         last = JOBS - 1
         for h in range(last - 2):
-            cap(h + 1)
-            expo(h, r0=2 if h == 0 else 0)
+            if h > 0:
+                cap(h + 1)
+            if h > 1:
+                expo(h)
             weigh(h)
             if h > PAIRED:
                 quant_w(h - 1)
-            elif h > 0 and h % 2 == 0:
+            elif h > 4 and h % 2 == 0:
                 quant_w(h - 2, 0, 2 * QT)
             u = h // 2 + 3
             if 3 < u < UNITS:
@@ -340,9 +348,10 @@ def tile_rows_a_exp_mask_cap_kernel(tc, qT, kT, t, v, mask, out):
         quant_w(last - 2)
         second(last - 2)
         weigh(last - 1, half, QT)
+        quant_w(last - 1, 0, half)
         invert(2)
         divide(2, 0, 4, on_scalar=True)
-        quant_w(last - 1)
+        quant_w(last - 1, half, QT)
         second(last - 1)
         for q0 in range(0, QT, quarter):
             weigh(last, q0, q0 + quarter)

@@ -84,7 +84,7 @@ def tile_rows_a_exp_mask_cap_kernel(tc, qT, kT, t, v, mask, out):
                     nc.sync.dma_start(out=raw[g * ROWS : (g + 1) * ROWS], in_=rows)
 
         def load_k():
-            nc.sync.dma_start(out=k_raw[:], in_=k_view)
+            nc.sync.dma_start(out=k_raw[:], in_=k_view, max_dma_last_dim=4096)
 
         def load_m(j, n):
             raw = sbuf("m_raw%d" % j, [P, PACK, n * QT], F32)
@@ -261,8 +261,8 @@ def tile_rows_a_exp_mask_cap_kernel(tc, qT, kT, t, v, mask, out):
                     )
 
         load_k()
-        load_t()
         load_q(0, 1)
+        load_t()
         load_q(1, 2)
         load_m(0, 2)
         load_q(3, 1)
@@ -273,12 +273,12 @@ def tile_rows_a_exp_mask_cap_kernel(tc, qT, kT, t, v, mask, out):
             load_q(u, 1)
 
         copy_k(0, 0, P)
-        deal_t()
         copy_k(2, 0, P, on_scalar=True)
         copy_q(0, 1)
         quant_k(0)
         quant_q(0, 1)
         quant_k(1)
+        deal_t()
         quant_k(2)
         quant_k(3)
         turn_t()

@@ -111,15 +111,15 @@ def tile_rows_a_exp_mask_cap_kernel(tc, qT, kT, t, v, mask, out):
         def turn_t():
             nc.vector.transpose(out=t_sb[:], in_=t_dealt[:])
 
-        def copy_q(u, n):
+        def copy_q(u, q0=0, q1=QT, copy=nc.vector.tensor_copy):
             raw, x = q_raw[u]
-            nc.vector.tensor_copy(
-                out=q_bf[:, u * QT : (u + n) * QT, :].rearrange("p (c i) j -> p c j i", i=4),
-                in_=raw[:, :, x * QT : (x + n) * QT].rearrange("p j (c i) -> p c j i", i=4),
+            copy(
+                out=q_bf[:, u * QT + q0 : u * QT + q1, :].rearrange("p (c i) j -> p c j i", i=4),
+                in_=raw[:, :, x * QT + q0 : x * QT + q1].rearrange("p j (c i) -> p c j i", i=4),
             )
 
-        def quant_q(u, n):
-            cols = slice(u * QT, (u + n) * QT)
+        def quant_q(u, q0=0, q1=QT):
+            cols = slice(u * QT + q0, u * QT + q1)
             nc.vector.quantize_mx(
                 out=q_codes[:, cols].bitcast(FP8X4),
                 scales=q_scales[:, cols],
@@ -274,9 +274,11 @@ def tile_rows_a_exp_mask_cap_kernel(tc, qT, kT, t, v, mask, out):
 
         copy_k(0, 0, P)
         copy_k(2, 0, P, on_scalar=True)
-        copy_q(0, 1)
+        copy_q(0, 0, 64)
+        copy_q(0, 64, QT)
         quant_k(0)
-        quant_q(0, 1)
+        quant_q(0, 0, 64)
+        quant_q(0, 64, QT)
         quant_k(1)
         deal_t()
         quant_k(2)
@@ -289,18 +291,17 @@ def tile_rows_a_exp_mask_cap_kernel(tc, qT, kT, t, v, mask, out):
         cap(1, r0=2)
         expo(0)
         expo(1)
-        copy_q(1, 1)
-        copy_q(2, 1)
-        quant_q(1, 1)
+        copy_q(1)
+        copy_q(2)
+        quant_q(1)
         scores(1)
-        quant_q(2, 1)
+        quant_q(2)
         make_mt(0, 2)
-        copy_q(3, 1)
+        copy_q(3)
 
         chores = {
-            0: [lambda: quant_q(3, 1)],
-            1: [copy_v, lambda: quant_w(0, 0, 2 * QT)],
-            2: [quant_v],
+            0: [lambda: quant_q(3)],
+            1: [copy_v, lambda: quant_w(0, 0, 2 * QT), quant_v],
             3: [lambda: make_mt(2, 2), lambda: quant_w(2, 0, 2 * QT)],
             6: [lambda: invert(0)],
             7: [lambda: divide(0, 0, 2)],
@@ -322,7 +323,7 @@ def tile_rows_a_exp_mask_cap_kernel(tc, qT, kT, t, v, mask, out):
                 quant_w(h - 2, 0, 2 * QT)
             u = h // 2 + 3
             if 3 < u < UNITS:
-                (quant_q if h % 2 else copy_q)(u, 1)
+                (quant_q if h % 2 else copy_q)(u)
             for chore in chores.get(h, []):
                 chore()
             if h % 2 == 0 and h + 4 < JOBS:
@@ -347,13 +348,14 @@ def tile_rows_a_exp_mask_cap_kernel(tc, qT, kT, t, v, mask, out):
         weigh(last - 1, 0, half)
         quant_w(last - 2)
         second(last - 2)
-        weigh(last - 1, half, QT)
-        quant_w(last - 1, 0, half)
         invert(2)
         divide(2, 0, 4, on_scalar=True)
+        weigh(last - 1, half, QT)
+        quant_w(last - 1, 0, half)
+        weigh(last, 0, quarter)
         quant_w(last - 1, half, QT)
         second(last - 1)
-        for q0 in range(0, QT, quarter):
+        for q0 in range(quarter, QT, quarter):
             weigh(last, q0, q0 + quarter)
         invert(3)
         divide(3, 0, 2, on_scalar=True)

from contextlib import ExitStack

import concourse.mybir as mybir

F32 = mybir.dt.float32
BF16 = mybir.dt.bfloat16
U32 = mybir.dt.uint32
U8 = mybir.dt.uint8
FP8X4 = mybir.dt.float8_e4m3fn_x4
ACT = mybir.ActivationFunctionType
ALU = mybir.AluOpType

H, KV, D, NQ, N, E = 4, 2, 256, 512, 512, 128
CAP = 2.0
P = 128
PACK = 4
ROWS = D // PACK
QT = 128
FLOPS = 2 * H * N * NQ * D + 2 * H * NQ * N * E
PAIRS = ((1, 2), (0, 3))
UNITS = 8
JOBS = 2 * UNITS
QUAD = 32
PAIRED = 10
GROUPS = ((0, 1, 2, 3), (4, 5, 6, 7), (8, 9, 10, 11), (12, 13), (14,), (15,))


def tile_rows_a_exp_mask_cap_kernel(tc, qT, kT, t, v, mask, out):
    nc = tc.nc
    with ExitStack() as ctx:
        sb = ctx.enter_context(tc.tile_pool(name="sb", bufs=1))
        ps = ctx.enter_context(tc.psum_pool(name="ps", bufs=1))
        ctx.enter_context(tc.manual_schedule())

        def sbuf(name, shape, dtype):
            return sb.tile(shape, dtype, name=name, align_bytes=64)

        q_raw = {}
        m_raw = {}
        q_bf = sbuf("q_bf", [P, UNITS * QT, PACK], BF16)
        q_codes = sbuf("q_codes", [P, UNITS * QT], U32)
        q_scales = sbuf("q_scales", [P, UNITS * QT], U8)
        k_raw = sbuf("k_raw", [P, PACK, N], F32)
        k_bf = sbuf("k_bf", [P, PACK, P, PACK], BF16)
        k_codes = sbuf("k_codes", [P, PACK, P], U32)
        k_scales = sbuf("k_scales", [P, PACK, P], U8)
        t_rows = sbuf("t_rows", [P, P], F32)
        t_dealt = sbuf("t_dealt", [P, P], F32)
        t_sb = sbuf("t_sb", [P, P], F32)
        mt = [sbuf("mt%d" % j, [P, PACK, 2 * QT], F32) for j in range(2)]
        v_raw = sbuf("v_raw", [P, KV, PACK, E], F32)
        v_bf = sbuf("v_bf", [P, KV, E, PACK], BF16)
        v_codes = sbuf("v_codes", [P, KV * E], U32)
        v_scales = sbuf("v_scales", [P, KV * E], U8)
        th = [sbuf("th%d" % h, [P, PACK, QT], F32) for h in range(JOBS)]
        pr = [sbuf("pr%d" % h, [P, PACK, QT], F32) for h in range(JOBS)]
        w_bf = sbuf("w_bf", [P, JOBS * QT * PACK], BF16)
        w_codes = sbuf("w_codes", [P, JOBS * QT], U32)
        w_scales = sbuf("w_scales", [P, JOBS * QT], U8)

        place = {h: (gi, i) for gi, members in enumerate(GROUPS) for i, h in enumerate(members)}
        recip = [sbuf("recip%d" % gi, [P, len(members)], F32) for gi, members in enumerate(GROUPS)]
        res = [sbuf("res%d" % gi, [P, len(members), E], F32) for gi, members in enumerate(GROUPS)]
        s_bank = {}
        turn = [1, 1]
        y_bank = {}

        q_flat = qT.rearrange("h d q -> (h d) q")
        k_view = kT.rearrange("g (p j) n -> (g p) j n", j=PACK)
        m_view = mask.rearrange("(p r) q -> p r q", r=PACK)

        def load_q(u, n):
            raw = sbuf("q_raw%d" % u, [P, PACK, n * QT], F32)
            for x in range(n):
                q_raw[u + x] = (raw, x)
            cols = slice((u % 4) * QT, (u % 4 + n) * QT)
            lo, hi = PAIRS[u // 4]
            if hi == lo + 1:
                rows = q_flat[lo * D : (hi + 1) * D, cols].rearrange("(p j) q -> p j q", j=PACK)
                nc.sync.dma_start(out=raw[:], in_=rows)
            else:
                for g, head in enumerate(PAIRS[u // 4]):
                    rows = qT[head, :, cols].rearrange("(p j) q -> p j q", j=PACK)
                    nc.sync.dma_start(out=raw[g * ROWS : (g + 1) * ROWS], in_=rows)

        def load_k():
            nc.sync.dma_start(out=k_raw[:], in_=k_view, max_dma_last_dim=4096)

        def load_m(j, n):
            raw = sbuf("m_raw%d" % j, [P, PACK, n * QT], F32)
            for x in range(n):
                m_raw[j + x] = (raw, x)
            nc.sync.dma_start(out=raw[:], in_=m_view[:, :, j * QT : (j + n) * QT])

        def load_v():
            nc.sync.dma_start(
                out=v_raw[:].rearrange("p g r e -> p g (r e)"),
                in_=v.rearrange("g (p r) e -> p g (r e)", r=PACK),
            )

        def load_t():
            nc.vector.memset(t_rows[:], 0.0)
            nc.sync.dma_start(out=t_rows[0:P:QUAD, :], in_=t.rearrange("(g n) o -> g (n o)", n=P))

        def deal_t():
            nc.vector.tensor_copy(
                out=t_dealt[:].rearrange("p (r a) -> p r a", r=PACK),
                in_=t_rows[:].rearrange("p (a r) -> p r a", r=PACK),
            )

        def turn_t():
            nc.vector.transpose(out=t_sb[:], in_=t_dealt[:])

        def copy_q(u, q0=0, q1=QT, copy=nc.vector.tensor_copy):
            raw, x = q_raw[u]
            copy(
                out=q_bf[:, u * QT + q0 : u * QT + q1, :].rearrange("p (c i) j -> p c j i", i=4),
                in_=raw[:, :, x * QT + q0 : x * QT + q1].rearrange("p j (c i) -> p c j i", i=4),
            )

        def quant_q(u, q0=0, q1=QT):
            cols = slice(u * QT + q0, u * QT + q1)
            nc.vector.quantize_mx(
                out=q_codes[:, cols].bitcast(FP8X4),
                scales=q_scales[:, cols],
                in_=q_bf[:, cols, :].rearrange("p q j -> p (q j)"),
            )

        def copy_k(r0, s0, s1, on_scalar=False):
            dst = k_bf[:, r0 : r0 + 2, s0:s1, :].rearrange("p r s j -> p s j r")
            src = k_raw[:].rearrange("p j (s r) -> p s j r", r=PACK)[:, s0:s1, :, r0 : r0 + 2]
            if on_scalar:
                nc.scalar.copy(out=dst, in_=src)
            else:
                nc.vector.tensor_copy(out=dst, in_=src)

        def quant_k(r):
            nc.vector.quantize_mx(
                out=k_codes[:, r, :].bitcast(FP8X4),
                scales=k_scales[:, r, :],
                in_=k_bf[:, r].rearrange("p s j -> p (s j)"),
            )

        def make_mt(j, n):
            raw, x = m_raw[j]
            for r in range(PACK):
                nc.vector.tensor_scalar(
                    out=mt[j // 2][:, r, (j % 2) * QT : (j % 2 + n) * QT],
                    in0=raw[:, r, x * QT : (x + n) * QT],
                    scalar1=t_sb[:, r * QUAD : r * QUAD + 1],
                    scalar2=None,
                    op0=ALU.mult,
                )

        def copy_v():
            nc.vector.tensor_copy(
                out=v_bf[:].rearrange("p g (c i) r -> p g c r i", i=4),
                in_=v_raw[:].rearrange("p g r (c i) -> p g c r i", i=4),
            )

        def quant_v():
            nc.vector.quantize_mx(
                out=v_codes[:].bitcast(FP8X4),
                scales=v_scales[:],
                in_=v_bf[:].rearrange("p g e r -> p (g e r)"),
            )

        def take_bank(h, r0=0):
            g = h % KV
            turn[g] = 1 - turn[g]
            s_bank[h, r0] = ps.tile([P, PACK, QT], F32, name="s%d_%d" % (h, r0), tag="s%d%d" % (g, turn[g]))

        def scores(u):
            cols = slice(u * QT, (u + 1) * QT)
            for g in range(KV):
                take_bank(KV * u + g)
            for r in range(PACK):
                if u == 0 and r == 2:
                    for g in range(KV):
                        take_bank(g, 2)
                for g in range(KV):
                    h = KV * u + g
                    rows = slice(g * ROWS, (g + 1) * ROWS)
                    nc.tensor.matmul_mx(
                        out=s_bank[h, 2 if u == 0 and r >= 2 else 0][:, r, :],
                        lhsT=k_codes[rows, r, :].bitcast(FP8X4),
                        lhsT_scale=k_scales[rows, r, :],
                        rhs=q_codes[rows, cols].bitcast(FP8X4),
                        rhs_scale=q_scales[rows, cols],
                        start=True,
                        stop=True,
                    )

        def cap(h, q0=0, q1=QT, r0=0, r1=PACK):
            nc.scalar.activation(
                out=th[h][:, r0:r1, q0:q1], in_=s_bank[h, r0][:, r0:r1, q0:q1], func=ACT.Tanh, scale=1.0 / CAP
            )

        def expo(h, q0=0, q1=QT, r0=0, r1=PACK):
            nc.scalar.activation(out=pr[h][:, r0:r1, q0:q1], in_=th[h][:, r0:r1, q0:q1], func=ACT.Exp, scale=CAP)

        def weigh(h, q0=0, q1=QT):
            j = (h // KV) % 4
            first = (j % 2) * QT
            nc.vector.tensor_tensor(
                out=w_bf[:, (h * QT + q0) * PACK : (h * QT + q1) * PACK].rearrange("p (c i r) -> p c r i", i=2, r=PACK),
                in0=pr[h][:, :, q0:q1].rearrange("p r (c i) -> p c r i", i=2),
                in1=mt[j // 2][:, :, first + q0 : first + q1].rearrange("p r (c i) -> p c r i", i=2),
                op=ALU.mult,
            )

        def quant_w(h, q0=0, q1=QT):
            nc.vector.quantize_mx(
                out=w_codes[:, h * QT + q0 : h * QT + q1].bitcast(FP8X4),
                scales=w_scales[:, h * QT + q0 : h * QT + q1],
                in_=w_bf[:, (h * QT + q0) * PACK : (h * QT + q1) * PACK],
            )

        def second(h):
            gi, i = place[h]
            if gi not in y_bank:
                y_bank[gi] = ps.tile([P, 2 * KV, E], F32, name="y%d" % gi, tag="y%d" % (gi % 4))
            cols = slice((h % KV) * E, (h % KV + 1) * E)
            nc.tensor.matmul_mx(
                out=y_bank[gi][:, i, :],
                lhsT=w_codes[:, h * QT : (h + 1) * QT].bitcast(FP8X4),
                lhsT_scale=w_scales[:, h * QT : (h + 1) * QT],
                rhs=v_codes[:, cols].bitcast(FP8X4),
                rhs_scale=v_scales[:, cols],
                start=True,
                stop=True,
            )

        def invert(gi):
            n = len(GROUPS[gi])
            nc.vector.reciprocal(out=recip[gi][:], in_=y_bank[gi][:, 0:n, E - 1])

        def divide(gi, i0, n, on_scalar=False):
            if on_scalar:
                for x in range(i0, i0 + n):
                    nc.scalar.activation(
                        out=res[gi][:, x, :], in_=y_bank[gi][:, x, :], func=ACT.Copy, scale=recip[gi][:, x : x + 1]
                    )
            else:
                nc.vector.tensor_tensor(
                    out=res[gi][:, i0 : i0 + n, :],
                    in0=y_bank[gi][:, i0 : i0 + n, :],
                    in1=recip[gi][:, i0 : i0 + n].unsqueeze(2).to_broadcast([P, n, E]),
                    op=ALU.mult,
                )
            for i in range(i0, i0 + n, KV):
                u, g = divmod(GROUPS[gi][i], KV)
                rows = slice((u % 4) * QT, (u % 4 + 1) * QT)
                lo, hi = PAIRS[u // 4]
                if n == 1:
                    nc.sync.dma_start(out=out[PAIRS[u // 4][g], rows, :], in_=res[gi][:, 0, :])
                else:
                    nc.sync.dma_start(
                        out=out[lo : hi + 1 : hi - lo, rows, :].rearrange("g q e -> q g e"),
                        in_=res[gi][:, i : i + KV, :],
                    )

        load_k()
        load_q(0, 1)
        load_t()
        load_q(1, 2)
        load_m(0, 2)
        load_q(3, 1)
        load_v()
        load_q(4, 1)
        load_m(2, 2)
        for u in range(5, UNITS):
            load_q(u, 1)

        copy_k(0, 0, P)
        copy_k(2, 0, P, on_scalar=True)
        copy_q(0, 0, 64)
        copy_q(0, 64, QT)
        quant_k(0)
        quant_q(0, 0, 64)
        quant_q(0, 64, QT)
        quant_k(1)
        deal_t()
        quant_k(2)
        quant_k(3)
        turn_t()
        scores(0)
        cap(0, r1=2)
        cap(1, r1=2)
        cap(0, r0=2)
        cap(1, r0=2)
        expo(0)
        expo(1)
        copy_q(1)
        copy_q(2)
        quant_q(1)
        scores(1)
        quant_q(2)
        make_mt(0, 2)
        copy_q(3)

        chores = {
            0: [lambda: quant_q(3)],
            1: [copy_v, lambda: quant_w(0, 0, 2 * QT), quant_v],
            3: [lambda: make_mt(2, 2), lambda: quant_w(2, 0, 2 * QT)],
            6: [lambda: invert(0)],
            7: [lambda: divide(0, 0, 2)],
            9: [lambda: divide(0, 2, 2), lambda: invert(1)],
            10: [lambda: divide(1, 0, 2)],
            11: [lambda: divide(1, 2, 2)],
        }
        done = 0
        last = JOBS - 1
        for h in range(last - 2):
            if h > 0:
                cap(h + 1)
            if h > 1:
                expo(h)
            weigh(h)
            if h > PAIRED:
                quant_w(h - 1)
            elif h > 4 and h % 2 == 0:
                quant_w(h - 2, 0, 2 * QT)
            u = h // 2 + 3
            if 3 < u < UNITS:
                (quant_q if h % 2 else copy_q)(u)
            for chore in chores.get(h, []):
                chore()
            if h % 2 == 0 and h + 4 < JOBS:
                scores(h // 2 + 2)
            if h > PAIRED or (h >= 4 and h % 2 == 0):
                for x in range(done, h):
                    second(x)
                done = h
        half, quarter = QT // 2, QT // 4
        expo(last - 2)
        cap(last - 1, 0, half)
        cap(last - 1, half, QT)
        expo(last - 1, 0, half)
        expo(last - 1, half, QT)
        cap(last, 0, half)
        cap(last, half, QT)
        for q0 in range(0, QT, quarter):
            expo(last, q0, q0 + quarter)
        weigh(last - 2)
        quant_w(last - 3)
        second(last - 3)
        weigh(last - 1, 0, half)
        quant_w(last - 2)
        second(last - 2)
        invert(2)
        divide(2, 0, 4, on_scalar=True)
        weigh(last - 1, half, QT)
        quant_w(last - 1, 0, half)
        weigh(last, 0, quarter)
        quant_w(last - 1, half, QT)
        second(last - 1)
        for q0 in range(quarter, QT, quarter):
            weigh(last, q0, q0 + quarter)
        invert(3)
        divide(3, 0, 2, on_scalar=True)
        quant_w(last, 0, half)
        quant_w(last, half, QT)
        second(last)
        invert(4)
        divide(4, 0, 1, on_scalar=True)
        invert(5)
        divide(5, 0, 1)
